import numpy as np, ml_dtypes
CORES = [4,20,36,52,68,84,100,116,132,148,164,180,196,212,228,244]
N = 16
R, L = 8192, 2048
CAPP = 256
def entries(a): return a.T.reshape(-1)
def pack(v, P): return np.ascontiguousarray(np.asarray(v, np.int32).reshape(-1, P).T)
def lists(rng, how):
    n = N * L
    P = rng.permutation(np.repeat(np.arange(N * N), CAPP))[:n]
    if how == "full":
        a, b = rng.permutation(N)[:2]; o = rng.permutation(N * N); o = o[(o // N != a) & (o % N != b)]
        C = np.concatenate([N * a + rng.permutation(np.delete(np.arange(N), b)), [N * a + b], N * rng.permutation(np.delete(np.arange(N), a)) + b, o])[:n // CAPP]
        P = np.repeat(C, CAPP).reshape(N, L)[rng.permutation(N)].reshape(-1)
    h, g = P // N, P % N
    d = np.zeros(n, np.int64)
    for q in range(N): m = np.nonzero(g == q)[0]; d[m] = R * q + np.concatenate([[0, R - 1], 1 + rng.permutation(R - 2)])[:len(m)]
    s = R * h + rng.integers(0, R, n)
    if how == "fork": s = R * h + rng.integers(0, R, N)[h]
    if how == "chain":
        for q in range(N):
            m = np.nonzero(h == q)[0]; w = d[g == q]
            if len(w): s[m] = w[rng.integers(0, len(w), len(m))]
    if how == "gaps":
        z = rng.permutation(N)[:3]; k = (rng.random(n) < 0.5) | (np.arange(n) // L == z[0]) | (h == z[1]) | (g == z[2]); s[k] = -1; d[k] = -1
    return {"src": np.stack([pack(v, 16) for v in s.reshape(N, L)]), "dst": np.stack([pack(v, 16) for v in d.reshape(N, L)])}
def setup_inputs(rng):
    return dict({"tab": rng.standard_normal((N, 128, R), dtype=np.float32).astype(ml_dtypes.bfloat16)}, **lists(rng, "uniform"))
def setup_inputs_chain(rng):
    d = setup_inputs(rng); d.update(lists(rng, "chain"))
    for k in ("tab",): d[k] = (d[k].astype(np.float32) * 1048576.0).astype(d[k].dtype)
    return d
def setup_inputs_fork(rng):
    d = setup_inputs(rng); d.update(lists(rng, "fork"))
    for k in ("tab",): d[k] = (d[k].astype(np.float32) * (1 / 1024.0)).astype(d[k].dtype)
    return d
def setup_inputs_full(rng):
    d = setup_inputs(rng); d.update(lists(rng, "full"))
    return d
def setup_inputs_gaps(rng):
    d = setup_inputs(rng); d.update(lists(rng, "gaps"))
    return d
def check_inputs(x):
    bad = []; s, d = x["src"].reshape(-1), x["dst"].reshape(-1); k = d >= 0
    if s.min() < -1 or s.max() >= N * R or d.min() < -1 or d.max() >= N * R: bad.append("out of range")
    if ((s < 0) != (d < 0)).any(): bad.append("half a pair")
    if len(np.unique(d[k])) != int(k.sum()): bad.append("a column is written twice")
    if k.any() and int(np.bincount(s[k] // R * N + d[k] // R).max()) > CAPP: bad.append("more than CAPP pairs from one rank's part to one rank's part")
    return bad
def reference(tab, src, dst):
    A = np.concatenate(list(tab), axis=1); Y = A.copy()
    for r in range(N):
        s, d = entries(src[r]), entries(dst[r]); k = d >= 0
        Y[:, d[k]] = A[:, s[k]]
    return {"y": np.stack([Y[:, R * r:R * r + R] for r in range(N)])}

@@ -1,0 +1,382 @@
+from concourse.bass import DstId, RemoteDMATransfer
+from concourse.mybir import AluOpType, ActivationFunctionType
+
+N, R, CAPP = 16, 8192, 256
+NJ, C, K = 8, 32, 16
+ADD, MULT, MAX, EQ = AluOpType.add, AluOpType.mult, AluOpType.max, AluOpType.is_equal
+COPY = ActivationFunctionType.Copy
+
+SCRATCH = {
+    "lst": ("dram", [128, 32], "int32"),
+    "lin": ("dram", [256, 32], "int32"),
+    "st": ("sbuf", [128, 64], "int32"),
+    "uu": ("sbuf", [128, 64], "int32"),
+    "vv": ("sbuf", [128, 64], "int32"),
+    "key": ("sbuf", [128, 64], "float32"),
+    "vi": ("sbuf", [128, 64], "int32"),
+    "vf": ("sbuf", [128, 64], "float32"),
+    "wi": ("sbuf", [128, 64], "int32"),
+    "wf": ("sbuf", [128, 96], "float32"),
+    "ones": ("sbuf", [128, 1024], "bfloat16"),
+    "c256": ("sbuf", [128, 1024], "bfloat16"),
+    "ident": ("sbuf", [128, 128], "bfloat16"),
+    "tri": ("sbuf", [128, 128], "bfloat16"),
+    "rst": ("sbuf", [128, 512], "bfloat16"),
+    "iota_a": ("sbuf", [128, 256], "bfloat16"),
+    "iota_k": ("sbuf", [128, 16], "float32"),
+    "iota_l": ("sbuf", [128, 128], "bfloat16"),
+    "iota_b": ("sbuf", [128, 64], "float32"),
+    "iota_c": ("sbuf", [128, 512], "float32"),
+    "pidx": ("sbuf", [128, 8], "int32"),
+    "pidf": ("sbuf", [128, 8], "float32"),
+    "sel_lo": ("sbuf", [128, 1024], "bfloat16"),
+    "sel_hi": ("sbuf", [128, 1024], "bfloat16"),
+    "oh_a": ("sbuf", [128, 32 * 256], "bfloat16"),
+    "oh_b": ("sbuf", [128, 32 * 32], "bfloat16"),
+    "oh_l": ("sbuf", [128, 32 * 128], "bfloat16"),
+    "oh_c": ("sbuf", [128, 32 * 128], "bfloat16"),
+    "xs": ("sbuf", [128, 64], "bfloat16"),
+    "xd": ("sbuf", [128, 128], "bfloat16"),
+    "xs_in": ("sbuf", [128, 8 * 64], "bfloat16"),
+    "xd_in": ("sbuf", [128, 8 * 128], "bfloat16"),
+    "ts": ("sbuf", [128, 64], "bfloat16"),
+    "td": ("sbuf", [128, 128], "bfloat16"),
+    "off_s": ("sbuf", [128, 256], "uint16"),
+    "inv_f": ("sbuf", [128, 512], "float32"),
+    "off_d": ("sbuf", [128, 512], "uint16"),
+    "win": ("sbuf", [128, R + N * CAPP], "bfloat16"),
+    "gat": ("sbuf", [128, N * CAPP], "bfloat16"),
+    "out": ("sbuf", [128, R], "bfloat16"),
+}
+for _r in ("s", "d"):
+    SCRATCH["m_" + _r] = ("sbuf", [128, 512], "bfloat16")
+    SCRATCH["q_" + _r] = ("sbuf", [128, 512], "bfloat16")
+    SCRATCH["z_" + _r] = ("sbuf", [128, 512], "bfloat16")
+    SCRATCH["w_" + _r] = ("sbuf", [128, 512], "bfloat16")
+    SCRATCH["cnt_" + _r] = ("sbuf", [128, 16], "bfloat16")
+    SCRATCH["cin_" + _r] = ("sbuf", [128, 8 * 16], "bfloat16")
+    SCRATCH["pos_" + _r] = ("sbuf", [128, 32], "float32")
+    SCRATCH["pb_base_" + _r] = ("psum", [128, 512], "float32")
+    SCRATCH["pb_pos_" + _r] = ("psum", [128, 512], "float32")
+for _b in ("pb_x0", "pb_x1", "pb_sum", "pb_wrap"):
+    SCRATCH[_b] = ("psum", [128, 512], "float32")
+
+NCH = 4
+SEMAPHORES = ["qv", "qa", "qp", "qg", "lcopy", "lsent", "la0", "la1", "ld", "loc", "c_s", "c_d", "x_s", "x_d", "tb", "arr",
+              "ys", "tl0", "tl1", "tl2", "tl3"]
+
+
+def bits(m):
+    return [b for b in range(16) if (m >> b) & 1]
+
+
+def rank_program(g, core, T, topo):
+    def chip_of(c):
+        return (topo.host(c), topo.chip(c))
+
+    total = 0
+    ncores = 256
+    mine = [r for r in range(N) if chip_of(T.cores[r]) == chip_of(core)]
+    if not mine:
+        return
+    rank = mine[0]
+
+    def layout(r):
+        me = T.cores[r]
+        cs = [c for c in range(ncores) if chip_of(c) == chip_of(me)]
+        far = [c for c in cs if topo.die(c) != topo.die(me)][0]
+        return [c for c in cs if c not in (me, far)] + [far, me]
+
+    lay = layout(rank)
+    j = lay.index(core)
+    main, far = lay[NJ - 1], lay[NJ - 2]
+    is_main, is_far = core == main, core == far
+    sender = is_main or is_far
+    S = T.sem
+    Q = {"v": g.vector, "a": g.scalar, "p": g.tensor, "g": g}
+    cnt = {"v": 0, "a": 0, "p": 0, "g": 0}
+    seen = {}
+
+    def run(q, ins):
+        ins.then_inc(S["q" + q], 1)
+        cnt[q] += 1
+        return (q, cnt[q])
+
+    def need(q, *toks):
+        best = {}
+        for t in toks:
+            if t is not None:
+                best[t[0]] = max(best.get(t[0], 0), t[1])
+        for s, n in best.items():
+            if seen.get((q, s), 0) < n:
+                Q[q].wait_ge(S["q" + s], n)
+                seen[(q, s)] = n
+
+    def did(d):
+        rid, pid = topo.addr(d, core)
+        return DstId(rid=rid, pnc=pid)
+
+    def mask_to(dsts, n, first=0):
+        m = 0xFFFF
+        for d in dsts:
+            m &= topo.mask(core, d)
+        b = bits(m)[first:first + n]
+        return sum(1 << x for x in b)
+
+    loc = [0]
+    E = 8
+
+    def send(src, dst, dsts, sem, local=None, n=E):
+        mask = mask_to(dsts, n)
+        g.remote_dma_fused([RemoteDMATransfer(dst_ids=[did(d) for d in dsts], dma_engine_mask=mask, remote_sem=sem,
+                                              srcs=[src], dsts=[dst for _ in dsts], alu_op=0)],
+                           local_sem=S.loc if local is None else local)
+        if local is None:
+            loc[0] += n
+
+    v, a, p = g.vector, g.scalar, g.tensor
+    last = NJ - 1
+
+    if is_main:
+        g.sync.dma_start(T.lst[0:64, :], T.src[:]).then_inc(S.lcopy, 16)
+        g.scalar.dma_start(T.lst[64:128, :], T.dst[:]).then_inc(S.lcopy, 16)
+    t_ones = run("v", v.memset(T.ones[:], 1.0))
+    k_k = run("g", g.iota(T.iota_k[:], [[1, K]], 32 * rank, 0, allow_small_or_imprecise_dtypes=True))
+    k_a = run("g", g.iota(T.iota_a[:], [[16, 2], [32, 8], [1, 16]], 1, 0, allow_small_or_imprecise_dtypes=True))
+    need("g", t_ones)
+    k_i = run("g", g.affine_select(T.ident[:], T.ones[:, 0:128], [[-1, 128]], EQ, 0.0, 0, 1))
+    if is_main:
+        jl = rank // 2
+        dsts = [layout(h)[jl] for h in range(N)]
+        dsts = [d for d in dsts if d != core]
+        g.wait_ge(S.lcopy, 32)
+        send(T.lst[:], T.lin[128 * (rank % 2):128 * (rank % 2) + 128, :], dsts, S["la%d" % (rank % 2)], local=S.lsent)
+    k_t = run("g", g.affine_select(T.tri[:], T.ones[:, 0:128], [[1, 128]], AluOpType.is_gt, 0.0, 0, -1))
+    k_r = run("g", g.affine_select(T.rst[:], T.ones[:, 0:512], [[0, K], [1, C]], AluOpType.not_equal, 0.0, 0, 0))
+    k_l = run("g", g.iota(T.iota_l[:], [[1, 128]], 0, 0, allow_small_or_imprecise_dtypes=True))
+    k_b = run("g", g.iota(T.iota_b[:], [[1, 64]], 64 * rank, 0, allow_small_or_imprecise_dtypes=True))
+    if sender:
+        t_256 = run("v", v.memset(T.c256[:], 256.0))
+    for k in range(2):
+        q = g.sync if k == 0 else g.scalar
+        own = is_main and rank == 2 * j + k
+        if own:
+            s_in, d_in = T.src[:], T.dst[:]
+        else:
+            q.wait_ge(S["la%d" % k], E)
+            s_in, d_in = T.lin[128 * k:128 * k + 64, :], T.lin[128 * k + 64:128 * k + 128, :]
+        q.dma_start(T.st[64 * k:64 * k + 64, 0:32], s_in).then_inc(S.ld, 16)
+        q.dma_start(T.st[64 * k:64 * k + 64, 32:64], d_in).then_inc(S.ld, 16)
+    if is_main:
+        w = R // NCH
+        g.sync.wait_ge(S.lsent, E)
+        for i in range(NCH):
+            g.sync.dma_start(T.win[:, w * i:w * i + w], T.tab[:, w * i:w * i + w]).then_inc(S["tl%d" % i], 16)
+        for i in range(NCH):
+            g.wait_ge(S["tl%d" % i], 16)
+            send(T.win[:, w * i:w * i + w], T.win[:, w * i:w * i + w], [far], S.tb, n=16)
+    if sender:
+        pat = [[-16, 8], [0, 8], [-1, 16]]
+        k_lo = run("g", g.affine_select(T.sel_lo[:], T.ones[:], pat, EQ, 0.0, 0, 1))
+        need("g", t_256)
+        k_hi = run("g", g.affine_select(T.sel_hi[:], T.c256[:], pat, EQ, 0.0, 0, 1))
+    if is_main:
+        k_p = run("g", g.iota(T.pidx[:], [[0, 8]], 0, 1))
+        k_c = run("g", g.iota(T.iota_c[:], [[16, 8], [128, 64]], 1, 0, allow_small_or_imprecise_dtypes=True))
+
+    v.wait_ge(S.ld, 64)
+    t1 = run("v", v.tensor_scalar(T.uu[:], T.st[:], 8, 480, AluOpType.arith_shift_right, AluOpType.bitwise_and))
+    t2 = run("v", v.tensor_scalar(T.vv[:], T.st[:], 13, None, AluOpType.arith_shift_right))
+    need("v", t1, t2)
+    run("v", v.tensor_tensor(T.key[:, 0:32], T.uu[:, 0:32], T.vv[:, 32:64], ADD))
+    t_key = run("v", v.tensor_tensor(T.key[:, 32:64], T.uu[:, 32:64], T.vv[:, 0:32], ADD))
+
+    def counts(r):
+        m, qq, c0 = T["m_" + r], T["q_" + r], 0 if r == "s" else 32
+        need("v", t_key, k_k)
+        for c in range(C):
+            t = run("v", v.tensor_scalar(m[:, c::C], T.iota_k[:], T.key[:, c0 + c:c0 + c + 1], None, EQ))
+        need("v", t, k_r)
+        t_q = run("v", v.tensor_tensor_scan(qq[:], T.rst[:], m[:], 0.0, MULT, ADD))
+        need("v", t_q)
+        t_c = run("v", v.tensor_copy(T["cnt_" + r][:], qq[:, C - 1::C]))
+        if j < last:
+            need("g", t_c)
+            send(T["cnt_" + r][:], T["cin_" + r][:, K * j:K * j + K], lay[j + 1:], S["c_" + r])
+        return t, t_c
+
+    def inner(r):
+        t_z = run("v", v.tensor_tensor(T["z_" + r][:], T["q_" + r][:], T["m_" + r][:], MULT))
+        need("p", t_z, k_i)
+        for k in range(K):
+            p_t = run("p", p.matmul(T["pb_pos_" + r][:, 0:C], T.ident[:], T["z_" + r][:, C * k:C * k + C], k == 0, False))
+        return p_t
+
+    def slots(r, t_c):
+        base, pos = T["pb_base_" + r], T["pb_pos_" + r]
+        need("p", t_c, k_t, t_ones)
+        p_b = run("p", p.matmul(base[:, 0:K], T.tri[:], T["cnt_" + r][:], True, j == 0))
+        if j:
+            p.wait_ge(S["c_" + r], E * j)
+            for i in range(j):
+                p_b = run("p", p.matmul(base[:, 0:K], T.ones[:, 0:128], T["cin_" + r][:, K * i:K * i + K], False, i == j - 1))
+        need("v", p_b)
+        for k in range(K):
+            t = run("v", v.tensor_scalar(T["w_" + r][:, C * k:C * k + C], T["m_" + r][:, C * k:C * k + C], base[:, k:k + 1],
+                                         None, MULT))
+            need("p", t)
+            p_t = run("p", p.matmul(pos[:, 0:C], T.ident[:], T["w_" + r][:, C * k:C * k + C], False, k == K - 1))
+        need("v", p_t)
+        return run("v", v.tensor_copy(T["pos_" + r][:], pos[:, 0:C]))
+
+    t_m, t_cs = counts("s")
+    run("v", v.tensor_scalar(T.vi[:, 0:32], T.st[:, 0:32], 255, None, AluOpType.bitwise_and))
+    t1 = run("v", v.tensor_scalar(T.vi[:, 32:64], T.st[:, 0:32], 8, 31, AluOpType.arith_shift_right, AluOpType.bitwise_and))
+    need("v", t1)
+    t_vf = run("v", v.tensor_copy(T.vf[:], T.vi[:]))
+    need("a", t_vf, t_m)
+    for c in range(C):
+        a_b = run("a", a.activation(T.oh_b[:, 32 * c:32 * c + 16], T.m_s[:, c::C], COPY, scale=T.vf[:, c:c + 1]))
+    inner("s")
+    need("v", t_vf)
+    for c in range(C):
+        t_b = run("v", v.tensor_scalar(T.oh_b[:, 32 * c + 16:32 * c + 32], T.iota_k[:], T.key[:, c:c + 1],
+                                       T.vf[:, 32 + c:33 + c], EQ, MULT))
+    t_pos = slots("s", t_cs)
+    need("v", t_pos, k_a)
+    need("p", a_b, t_b)
+    for c in range(C):
+        t = run("v", v.tensor_scalar(T.oh_a[:, 256 * c:256 * c + 256], T.iota_a[:], T.pos_s[:, c:c + 1], None, EQ))
+        need("p", t)
+        for b, xb in enumerate((T.pb_x0, T.pb_x1)):
+            p_x = run("p", p.matmul(xb[:, 0:32], T.oh_a[:, 256 * c + 128 * b:256 * c + 128 * b + 128],
+                                    T.oh_b[:, 32 * c:32 * c + 32], c == 0, c == C - 1))
+    need("v", p_x)
+    need("a", p_x)
+    for kind in range(2):
+        t_x = run("v", v.tensor_copy(T.xs[:, 32 * kind:32 * kind + 16], T.pb_x0[:, 16 * kind:16 * kind + 16]))
+        a_x = run("a", a.activation(T.xs[:, 32 * kind + 16:32 * kind + 32], T.pb_x1[:, 16 * kind:16 * kind + 16], COPY))
+    need("g", t_x, a_x)
+    send(T.xs[:], T.xs_in[:, 64 * j:64 * j + 64], [d for d in (far, main) if d != core], S.x_s)
+
+    t_md, t_cd = counts("d")
+    inner("d")
+
+    def total_of(x_in, x_own, width, sem):
+        need("p", t_x, a_x)
+        p.wait_ge(sem, E * (NJ - 1))
+        for i in range(NJ):
+            src = x_own[:] if i == j else x_in[:, width * i:width * i + width]
+            t = run("p", p.matmul(T.pb_sum[:, 0:width], T.ident[:], src, i == 0, i == NJ - 1))
+        return t
+
+    if sender:
+        pt = total_of(T.xs_in, T.xs, 64, S.x_s)
+        need("v", pt)
+        t_t = run("v", v.tensor_copy(T.ts[:], T.pb_sum[:, 0:64]))
+        need("p", t_t, k_lo, k_hi)
+        for k in range(8):
+            run("p", p.matmul(T.pb_wrap[:, 32 * k:32 * k + 32], T.sel_lo[:, 128 * k:128 * k + 128], T.ts[:, 0:32], True, False))
+            pt = run("p", p.matmul(T.pb_wrap[:, 32 * k:32 * k + 32], T.sel_hi[:, 128 * k:128 * k + 128], T.ts[:, 32:64],
+                                   False, True))
+        need("v", pt)
+        half = [x for x in range(N) if (x // 8 == rank // 8) == is_main]
+        first = rank % 8 + 1
+        peers = half[first:] + half[:first]
+        for x in peers[0:2]:
+            t = run("v", v.tensor_copy(T.off_s[:, 16 * x:16 * x + 16], T.pb_wrap[:, x:256:16]))
+        if is_main:
+            for q in (v, a):
+                for i in range(NCH):
+                    q.wait_ge(S["tl%d" % i], 16)
+        else:
+            v.wait_ge(S.tb, 16 * NCH)
+            a.wait_ge(S.tb, 16 * NCH)
+        toks = {}
+        for i in range(0, 8, 2):
+            for x, qn in ((peers[i], "v"), (peers[i + 1], "a")):
+                dst = T.win[:, R + CAPP * x:R + CAPP * x + CAPP] if x == rank else T.gat[:, CAPP * x:CAPP * x + CAPP]
+                src = T.win[:, 0:R].indirect(T.off_s[:, 16 * x:16 * x + 16])
+                need(qn, t)
+                if qn == "v":
+                    toks[x] = run("v", v.tensor_copy(dst, src))
+                else:
+                    toks[x] = run("a", a.activation(dst, src, COPY))
+            for x in peers[i + 2:i + 4]:
+                t = run("v", v.tensor_copy(T.off_s[:, 16 * x:16 * x + 16], T.pb_wrap[:, x:256:16]))
+        for i in range(0, 8, 4):
+            grp = [x for x in peers[i:i + 4] if x != rank]
+            need("g", *[toks[x] for x in grp])
+            tr = []
+            for i2, x in enumerate(grp):
+                d = T.cores[x]
+                tr.append(RemoteDMATransfer(dst_ids=[did(d)], dma_engine_mask=mask_to([d], 2, 2 * i2), remote_sem=S.arr,
+                                            srcs=[T.gat[:, CAPP * x:CAPP * x + CAPP]],
+                                            dsts=[T.win[:, R + CAPP * rank:R + CAPP * rank + CAPP]], alu_op=0))
+                loc[0] += 2
+            g.remote_dma_fused(tr, local_sem=S.loc)
+
+    t1 = run("v", v.tensor_scalar(T.wi[:, 0:32], T.st[:, 32:64], 127, None, AluOpType.bitwise_and))
+    t2 = run("v", v.tensor_scalar(T.wi[:, 32:64], T.st[:, 32:64], 7, None, AluOpType.arith_shift_right))
+    need("v", t1, t2)
+    run("v", v.tensor_copy(T.wf[:, 0:64], T.wi[:]))
+    t1 = run("v", v.tensor_scalar(T.wf[:, 64:96], T.vv[:, 0:32], R // 256, None, ADD))
+    need("v", t1, k_l, k_b)
+    for c in range(C):
+        run("v", v.tensor_scalar(T.oh_l[:, 128 * c:128 * c + 128], T.iota_l[:], T.wf[:, c:c + 1], None, EQ))
+        t_hi = run("v", v.tensor_scalar(T.oh_c[:, 128 * c + 64:128 * c + 128], T.iota_b[:], T.wf[:, 32 + c:33 + c],
+                                        T.wf[:, 64 + c:65 + c], EQ, MULT))
+    t_pos = slots("d", t_cd)
+    need("v", t_pos)
+    need("p", t_x)
+    for c in range(C):
+        t = run("v", v.tensor_scalar(T.oh_c[:, 128 * c:128 * c + 64], T.iota_b[:], T.wf[:, 32 + c:33 + c],
+                                     T.pos_d[:, c:c + 1], EQ, MULT))
+        need("p", t)
+        p_x = run("p", p.matmul(T.pb_x0[:, 0:128], T.oh_l[:, 128 * c:128 * c + 128], T.oh_c[:, 128 * c:128 * c + 128],
+                                c == 0, c == C - 1))
+    need("v", p_x)
+    t_x = run("v", v.tensor_copy(T.xd[:], T.pb_x0[:, 0:128]))
+    if not is_main:
+        need("g", t_x)
+        send(T.xd[:], T.xd_in[:, 128 * j:128 * j + 128], [main], S.x_d)
+
+    if is_main:
+        need("v", k_p, k_c)
+        t = run("v", v.tensor_scalar(T.pidx[:], T.pidx[:], 15, None, AluOpType.bitwise_and))
+        need("v", t)
+        t = run("v", v.tensor_copy(T.pidf[:], T.pidx[:]))
+        need("v", t)
+        t_ic = run("v", v.tensor_scalar(T.iota_c[:], T.iota_c[:], T.pidf[:, 0:1], None, ADD))
+        need("p", t_t)
+        pt = total_of(T.xd_in, T.xd, 128, S.x_d)
+        need("v", pt)
+        t = run("v", v.tensor_copy(T.td[:], T.pb_sum[:, 0:128]))
+        need("p", t)
+        for k in range(8):
+            run("p", p.matmul(T.pb_wrap[:, 64 * k:64 * k + 64], T.sel_lo[:, 128 * k:128 * k + 128], T.td[:, 0:64], True, False))
+            pt = run("p", p.matmul(T.pb_wrap[:, 64 * k:64 * k + 64], T.sel_hi[:, 128 * k:128 * k + 128], T.td[:, 64:128],
+                                   False, True))
+        need("v", pt, t_ic)
+        t = run("v", v.tensor_tensor(T.inv_f[:], T.pb_wrap[:], T.iota_c[:], MAX))
+        need("v", t)
+        for k in range(8):
+            t = run("v", v.tensor_scalar(T.off_d[:, k::8], T.inv_f[:, 64 * k:64 * k + 64], -1.0, None, ADD))
+        v.wait_ge(S.arr, 2 * (N - 1))
+        a.wait_ge(S.arr, 2 * (N - 1))
+        need("v", t, toks[peers[7]])
+        need("a", t, toks[peers[7]])
+        wy, ky = 1024, 64
+        ny = R // wy
+        for i in range(ny):
+            src = T.win[:].indirect(T.off_d[:, ky * i:ky * i + ky])
+            dst = T.out[:, wy * i:wy * i + wy]
+            t = run("v", v.tensor_copy(dst, src)) if i % 2 == 0 else run("a", a.activation(dst, src, COPY))
+            g.sync.wait_ge(S["q" + t[0]], t[1])
+            g.sync.dma_start(T.y[:, wy * i:wy * i + wy], dst).then_inc(S.ys, 16)
+        g.wait_ge(S.ys, 16 * ny)
+
+    for q in ("v", "a", "p", "g"):
+        if cnt[q]:
+            g.wait_ge(S["q" + q], cnt[q])
+    g.wait_ge(S.loc, loc[0])

@@ -3,42 +3,56 @@ from concourse.mybir import AluOpType, ActivationFunctionType
 
 N, R, CAPP = 16, 8192, 256
 NJ, C, K = 8, 32, 16
+ND = 4
+NCH = 4
+E, EC = 8, 16
 ADD, MULT, MAX, EQ = AluOpType.add, AluOpType.mult, AluOpType.max, AluOpType.is_equal
+SR, AN = AluOpType.arith_shift_right, AluOpType.bitwise_and
 COPY = ActivationFunctionType.Copy
+Y_CHUNKS = (256, 768, 1024, 1024, 768, 256)
 
 SCRATCH = {
     "lst": ("dram", [128, 32], "int32"),
     "lin": ("dram", [256, 32], "int32"),
     "st": ("sbuf", [128, 64], "int32"),
-    "uu": ("sbuf", [128, 64], "int32"),
-    "vv": ("sbuf", [128, 64], "int32"),
-    "key": ("sbuf", [128, 64], "float32"),
-    "vi": ("sbuf", [128, 64], "int32"),
-    "vf": ("sbuf", [128, 64], "float32"),
-    "wi": ("sbuf", [128, 64], "int32"),
-    "wf": ("sbuf", [128, 96], "float32"),
+    "uu": ("sbuf", [128, 32], "int32"),
+    "vv": ("sbuf", [128, 32], "int32"),
+    "key": ("sbuf", [128, 32], "float32"),
+    "vi": ("sbuf", [128, 128], "int32"),
+    "vf": ("sbuf", [128, 128], "float32"),
+    "hot": ("sbuf", [128, 512], "bfloat16"),
+    "inc": ("sbuf", [128, 512], "bfloat16"),
+    "zz": ("sbuf", [128, 512], "bfloat16"),
+    "ww": ("sbuf", [128, 512], "bfloat16"),
+    "cnt": ("sbuf", [128, 16], "bfloat16"),
+    "cin": ("sbuf", [128, 8 * 16], "bfloat16"),
+    "pos": ("sbuf", [128, 32], "float32"),
     "ones": ("sbuf", [128, 1024], "bfloat16"),
     "c256": ("sbuf", [128, 1024], "bfloat16"),
     "ident": ("sbuf", [128, 128], "bfloat16"),
     "tri": ("sbuf", [128, 128], "bfloat16"),
     "rst": ("sbuf", [128, 512], "bfloat16"),
     "iota_a": ("sbuf", [128, 256], "bfloat16"),
-    "iota_k": ("sbuf", [128, 16], "float32"),
     "iota_l": ("sbuf", [128, 128], "bfloat16"),
-    "iota_b": ("sbuf", [128, 64], "float32"),
+    "iota_b": ("sbuf", [128, 64], "bfloat16"),
     "iota_c": ("sbuf", [128, 512], "float32"),
     "pidx": ("sbuf", [128, 8], "int32"),
     "pidf": ("sbuf", [128, 8], "float32"),
     "sel_lo": ("sbuf", [128, 1024], "bfloat16"),
     "sel_hi": ("sbuf", [128, 1024], "bfloat16"),
     "oh_a": ("sbuf", [128, 32 * 256], "bfloat16"),
-    "oh_b": ("sbuf", [128, 32 * 32], "bfloat16"),
-    "oh_l": ("sbuf", [128, 32 * 128], "bfloat16"),
-    "oh_c": ("sbuf", [128, 32 * 128], "bfloat16"),
+    "oh_b": ("sbuf", [128, 4 * 512], "bfloat16"),
+    "oh_l": ("sbuf", [128, 8 * 128], "bfloat16"),
+    "oh_c": ("sbuf", [128, 8 * 128], "bfloat16"),
     "xs": ("sbuf", [128, 64], "bfloat16"),
-    "xd": ("sbuf", [128, 128], "bfloat16"),
+    "xt": ("sbuf", [128, 64], "bfloat16"),
     "xs_in": ("sbuf", [128, 8 * 64], "bfloat16"),
-    "xd_in": ("sbuf", [128, 8 * 128], "bfloat16"),
+    "xt_in": ("sbuf", [128, 8 * 64], "bfloat16"),
+    "dm": ("sbuf", [128, 16], "bfloat16"),
+    "din": ("sbuf", [128, 16], "bfloat16"),
+    "df": ("sbuf", [128, 16], "float32"),
+    "xd": ("sbuf", [128, 128], "bfloat16"),
+    "xd_in": ("sbuf", [128, 4 * 128], "bfloat16"),
     "ts": ("sbuf", [128, 64], "bfloat16"),
     "td": ("sbuf", [128, 128], "bfloat16"),
     "off_s": ("sbuf", [128, 256], "uint16"),
@@ -48,22 +62,11 @@ SCRATCH = {
     "gat": ("sbuf", [128, N * CAPP], "bfloat16"),
     "out": ("sbuf", [128, R], "bfloat16"),
 }
-for _r in ("s", "d"):
-    SCRATCH["m_" + _r] = ("sbuf", [128, 512], "bfloat16")
-    SCRATCH["q_" + _r] = ("sbuf", [128, 512], "bfloat16")
-    SCRATCH["z_" + _r] = ("sbuf", [128, 512], "bfloat16")
-    SCRATCH["w_" + _r] = ("sbuf", [128, 512], "bfloat16")
-    SCRATCH["cnt_" + _r] = ("sbuf", [128, 16], "bfloat16")
-    SCRATCH["cin_" + _r] = ("sbuf", [128, 8 * 16], "bfloat16")
-    SCRATCH["pos_" + _r] = ("sbuf", [128, 32], "float32")
-    SCRATCH["pb_base_" + _r] = ("psum", [128, 512], "float32")
-    SCRATCH["pb_pos_" + _r] = ("psum", [128, 512], "float32")
-for _b in ("pb_x0", "pb_x1", "pb_sum", "pb_wrap"):
+for _b in ("pb_base", "pb_pos", "pb_x0", "pb_x1", "pb_sum", "pb_wrap"):
     SCRATCH[_b] = ("psum", [128, 512], "float32")
 
-NCH = 4
-SEMAPHORES = ["qv", "qa", "qp", "qg", "lcopy", "lsent", "la0", "la1", "ld", "loc", "c_s", "c_d", "x_s", "x_d", "tb", "arr",
-              "ys", "tl0", "tl1", "tl2", "tl3"]
+SEMAPHORES = ["qv", "qa", "qp", "qg", "lcopy", "lsent", "la0", "la1", "ld", "loc", "cn", "x_s", "x_t", "dd", "x_d", "tb",
+              "arr", "ys", "tl0", "tl1", "tl2", "tl3"]
 
 
 def bits(m):
@@ -74,8 +77,6 @@ def rank_program(g, core, T, topo):
     def chip_of(c):
         return (topo.host(c), topo.chip(c))
 
-    total = 0
-    ncores = 256
     mine = [r for r in range(N) if chip_of(T.cores[r]) == chip_of(core)]
     if not mine:
         return
@@ -83,17 +84,18 @@ def rank_program(g, core, T, topo):
 
     def layout(r):
         me = T.cores[r]
-        cs = [c for c in range(ncores) if chip_of(c) == chip_of(me)]
+        cs = [c for c in range(256) if chip_of(c) == chip_of(me)]
         far = [c for c in cs if topo.die(c) != topo.die(me)][0]
         return [c for c in cs if c not in (me, far)] + [far, me]
 
     lay = layout(rank)
-    j = lay.index(core)
+    j, last = lay.index(core), NJ - 1
     main, far = lay[NJ - 1], lay[NJ - 2]
     is_main, is_far = core == main, core == far
     sender = is_main or is_far
     S = T.sem
-    Q = {"v": g.vector, "a": g.scalar, "p": g.tensor, "g": g}
+    v, a, p = g.vector, g.scalar, g.tensor
+    Q = {"v": v, "a": a, "p": p, "g": g, "s": g.sync}
     cnt = {"v": 0, "a": 0, "p": 0, "g": 0}
     seen = {}
 
@@ -105,8 +107,7 @@ def rank_program(g, core, T, topo):
     def need(q, *toks):
         best = {}
         for t in toks:
-            if t is not None:
-                best[t[0]] = max(best.get(t[0], 0), t[1])
+            best[t[0]] = max(best.get(t[0], 0), t[1])
         for s, n in best.items():
             if seen.get((q, s), 0) < n:
                 Q[q].wait_ge(S["q" + s], n)
@@ -116,51 +117,49 @@ def rank_program(g, core, T, topo):
         rid, pid = topo.addr(d, core)
         return DstId(rid=rid, pnc=pid)
 
-    def mask_to(dsts, n, first=0):
+    def engines(dsts, n, first=0):
         m = 0xFFFF
         for d in dsts:
             m &= topo.mask(core, d)
-        b = bits(m)[first:first + n]
-        return sum(1 << x for x in b)
+        return sum(1 << x for x in bits(m)[first:first + n])
 
     loc = [0]
-    E = 8
 
-    def send(src, dst, dsts, sem, local=None, n=E):
-        mask = mask_to(dsts, n)
-        g.remote_dma_fused([RemoteDMATransfer(dst_ids=[did(d) for d in dsts], dma_engine_mask=mask, remote_sem=sem,
-                                              srcs=[src], dsts=[dst for _ in dsts], alu_op=0)],
-                           local_sem=S.loc if local is None else local)
+    def move(src, dst, dsts, sem, n, first=0):
+        return RemoteDMATransfer(dst_ids=[did(d) for d in dsts], dma_engine_mask=engines(dsts, n, first), remote_sem=sem,
+                                 srcs=[src], dsts=[dst for _ in dsts], alu_op=0)
+
+    def send(parts, local=None):
+        g.remote_dma_fused([move(*x) for x in parts], local_sem=S.loc if local is None else local)
         if local is None:
-            loc[0] += n
+            loc[0] += sum(x[4] for x in parts)
 
-    v, a, p = g.vector, g.scalar, g.tensor
-    last = NJ - 1
+    def others(cs):
+        return [c for c in cs if c != core]
 
     if is_main:
         g.sync.dma_start(T.lst[0:64, :], T.src[:]).then_inc(S.lcopy, 16)
         g.scalar.dma_start(T.lst[64:128, :], T.dst[:]).then_inc(S.lcopy, 16)
     t_ones = run("v", v.memset(T.ones[:], 1.0))
-    k_k = run("g", g.iota(T.iota_k[:], [[1, K]], 32 * rank, 0, allow_small_or_imprecise_dtypes=True))
     k_a = run("g", g.iota(T.iota_a[:], [[16, 2], [32, 8], [1, 16]], 1, 0, allow_small_or_imprecise_dtypes=True))
     need("g", t_ones)
     k_i = run("g", g.affine_select(T.ident[:], T.ones[:, 0:128], [[-1, 128]], EQ, 0.0, 0, 1))
     if is_main:
-        jl = rank // 2
-        dsts = [layout(h)[jl] for h in range(N)]
-        dsts = [d for d in dsts if d != core]
+        k = rank % 2
+        dsts = others([layout(h)[rank // 2] for h in range(N)])
         g.wait_ge(S.lcopy, 32)
-        send(T.lst[:], T.lin[128 * (rank % 2):128 * (rank % 2) + 128, :], dsts, S["la%d" % (rank % 2)], local=S.lsent)
+        send([(T.lst[:], T.lin[128 * k:128 * k + 128, :], dsts, S["la%d" % k], E)], S.lsent)
     k_t = run("g", g.affine_select(T.tri[:], T.ones[:, 0:128], [[1, 128]], AluOpType.is_gt, 0.0, 0, -1))
     k_r = run("g", g.affine_select(T.rst[:], T.ones[:, 0:512], [[0, K], [1, C]], AluOpType.not_equal, 0.0, 0, 0))
-    k_l = run("g", g.iota(T.iota_l[:], [[1, 128]], 0, 0, allow_small_or_imprecise_dtypes=True))
-    k_b = run("g", g.iota(T.iota_b[:], [[1, 64]], 64 * rank, 0, allow_small_or_imprecise_dtypes=True))
+    if j < ND:
+        k_l = run("g", g.iota(T.iota_l[:], [[1, 128]], 0, 0, allow_small_or_imprecise_dtypes=True))
+        k_b = run("g", g.iota(T.iota_b[:], [[1, 64]], 1, 0, allow_small_or_imprecise_dtypes=True))
+        k_p = run("g", g.iota(T.pidx[:], [[0, 8]], 0, 1))
     if sender:
         t_256 = run("v", v.memset(T.c256[:], 256.0))
     for k in range(2):
-        q = g.sync if k == 0 else g.scalar
-        own = is_main and rank == 2 * j + k
-        if own:
+        q = g.sync if k == 0 or is_main else g.scalar
+        if is_main and rank == 2 * j + k:
             s_in, d_in = T.src[:], T.dst[:]
         else:
             q.wait_ge(S["la%d" % k], E)
@@ -174,7 +173,7 @@ def rank_program(g, core, T, topo):
             g.sync.dma_start(T.win[:, w * i:w * i + w], T.tab[:, w * i:w * i + w]).then_inc(S["tl%d" % i], 16)
         for i in range(NCH):
             g.wait_ge(S["tl%d" % i], 16)
-            send(T.win[:, w * i:w * i + w], T.win[:, w * i:w * i + w], [far], S.tb, n=16)
+            send([(T.win[:, w * i:w * i + w], T.win[:, w * i:w * i + w], [far], S.tb, 16)])
     if sender:
         pat = [[-16, 8], [0, 8], [-1, 16]]
         k_lo = run("g", g.affine_select(T.sel_lo[:], T.ones[:], pat, EQ, 0.0, 0, 1))
@@ -185,178 +184,185 @@ def rank_program(g, core, T, topo):
         k_c = run("g", g.iota(T.iota_c[:], [[16, 8], [128, 64]], 1, 0, allow_small_or_imprecise_dtypes=True))
 
     v.wait_ge(S.ld, 64)
-    t1 = run("v", v.tensor_scalar(T.uu[:], T.st[:], 8, 480, AluOpType.arith_shift_right, AluOpType.bitwise_and))
-    t2 = run("v", v.tensor_scalar(T.vv[:], T.st[:], 13, None, AluOpType.arith_shift_right))
+    t1 = run("v", v.tensor_scalar(T.uu[:], T.st[:, 0:32], 8, 480, SR, AN))
+    t2 = run("v", v.tensor_scalar(T.vv[:], T.st[:, 32:64], 13, None, SR))
     need("v", t1, t2)
-    run("v", v.tensor_tensor(T.key[:, 0:32], T.uu[:, 0:32], T.vv[:, 32:64], ADD))
-    t_key = run("v", v.tensor_tensor(T.key[:, 32:64], T.uu[:, 32:64], T.vv[:, 0:32], ADD))
-
-    def counts(r):
-        m, qq, c0 = T["m_" + r], T["q_" + r], 0 if r == "s" else 32
-        need("v", t_key, k_k)
-        for c in range(C):
-            t = run("v", v.tensor_scalar(m[:, c::C], T.iota_k[:], T.key[:, c0 + c:c0 + c + 1], None, EQ))
-        need("v", t, k_r)
-        t_q = run("v", v.tensor_tensor_scan(qq[:], T.rst[:], m[:], 0.0, MULT, ADD))
-        need("v", t_q)
-        t_c = run("v", v.tensor_copy(T["cnt_" + r][:], qq[:, C - 1::C]))
-        if j < last:
-            need("g", t_c)
-            send(T["cnt_" + r][:], T["cin_" + r][:, K * j:K * j + K], lay[j + 1:], S["c_" + r])
-        return t, t_c
-
-    def inner(r):
-        t_z = run("v", v.tensor_tensor(T["z_" + r][:], T["q_" + r][:], T["m_" + r][:], MULT))
-        need("p", t_z, k_i)
-        for k in range(K):
-            p_t = run("p", p.matmul(T["pb_pos_" + r][:, 0:C], T.ident[:], T["z_" + r][:, C * k:C * k + C], k == 0, False))
-        return p_t
-
-    def slots(r, t_c):
-        base, pos = T["pb_base_" + r], T["pb_pos_" + r]
-        need("p", t_c, k_t, t_ones)
-        p_b = run("p", p.matmul(base[:, 0:K], T.tri[:], T["cnt_" + r][:], True, j == 0))
-        if j:
-            p.wait_ge(S["c_" + r], E * j)
-            for i in range(j):
-                p_b = run("p", p.matmul(base[:, 0:K], T.ones[:, 0:128], T["cin_" + r][:, K * i:K * i + K], False, i == j - 1))
-        need("v", p_b)
-        for k in range(K):
-            t = run("v", v.tensor_scalar(T["w_" + r][:, C * k:C * k + C], T["m_" + r][:, C * k:C * k + C], base[:, k:k + 1],
-                                         None, MULT))
-            need("p", t)
-            p_t = run("p", p.matmul(pos[:, 0:C], T.ident[:], T["w_" + r][:, C * k:C * k + C], False, k == K - 1))
-        need("v", p_t)
-        return run("v", v.tensor_copy(T["pos_" + r][:], pos[:, 0:C]))
-
-    t_m, t_cs = counts("s")
-    run("v", v.tensor_scalar(T.vi[:, 0:32], T.st[:, 0:32], 255, None, AluOpType.bitwise_and))
-    t1 = run("v", v.tensor_scalar(T.vi[:, 32:64], T.st[:, 0:32], 8, 31, AluOpType.arith_shift_right, AluOpType.bitwise_and))
+    t = run("v", v.tensor_tensor(T.key[:], T.uu[:], T.vv[:], ADD))
+    need("v", t)
+    for k in range(K):
+        t_m = run("v", v.tensor_scalar(T.hot[:, C * k:C * k + C], T.key[:], float(32 * rank + k), None, EQ))
+    need("v", t_m, k_r)
+    t_q = run("v", v.tensor_tensor_scan(T.inc[:], T.rst[:], T.hot[:], 0.0, MULT, ADD))
+    need("v", t_q)
+    t_c = run("v", v.tensor_copy(T.cnt[:], T.inc[:, C - 1::C]))
+    if j < last:
+        need("g", t_c)
+        send([(T.cnt[:], T.cin[:, K * j:K * j + K], lay[j + 1:], S.cn, EC)])
+    run("v", v.tensor_scalar(T.vi[:, 0:32], T.st[:, 0:32], 255, None, AN))
+    run("v", v.tensor_scalar(T.vi[:, 32:64], T.st[:, 0:32], 8, 31, SR, AN))
+    run("v", v.tensor_scalar(T.vi[:, 64:96], T.st[:, 32:64], 127, None, AN))
+    t1 = run("v", v.tensor_scalar(T.vi[:, 96:128], T.st[:, 32:64], 7, 63, SR, AN))
     need("v", t1)
-    t_vf = run("v", v.tensor_copy(T.vf[:], T.vi[:]))
+    run("v", v.tensor_copy(T.vf[:, 0:96], T.vi[:, 0:96]))
+    t_vf = run("v", v.tensor_scalar(T.vf[:, 96:128], T.vi[:, 96:128], 1.0, None, ADD))
     need("a", t_vf, t_m)
+    a_b = []
     for c in range(C):
-        a_b = run("a", a.activation(T.oh_b[:, 32 * c:32 * c + 16], T.m_s[:, c::C], COPY, scale=T.vf[:, c:c + 1]))
-    inner("s")
+        for kind in (2, 3):
+            t = run("a", a.activation(T.oh_b[:, 512 * kind + c:512 * kind + 512:C], T.hot[:, c::C], COPY,
+                                      scale=T.vf[:, 32 * kind + c:32 * kind + c + 1]))
+        a_b.append(t)
+    t_z = run("v", v.tensor_tensor(T.zz[:], T.inc[:], T.hot[:], MULT))
     need("v", t_vf)
-    for c in range(C):
-        t_b = run("v", v.tensor_scalar(T.oh_b[:, 32 * c + 16:32 * c + 32], T.iota_k[:], T.key[:, c:c + 1],
-                                       T.vf[:, 32 + c:33 + c], EQ, MULT))
-    t_pos = slots("s", t_cs)
-    need("v", t_pos, k_a)
-    need("p", a_b, t_b)
-    for c in range(C):
-        t = run("v", v.tensor_scalar(T.oh_a[:, 256 * c:256 * c + 256], T.iota_a[:], T.pos_s[:, c:c + 1], None, EQ))
+    for kind in (0, 1):
+        for k in range(K):
+            t_b = run("v", v.tensor_tensor(T.oh_b[:, 512 * kind + C * k:512 * kind + C * k + C], T.hot[:, C * k:C * k + C],
+                                           T.vf[:, 32 * kind:32 * kind + 32], MULT))
+    need("p", t_z, k_i)
+    for k in range(K):
+        run("p", p.matmul(T.pb_pos[:, 0:C], T.ident[:], T.zz[:, C * k:C * k + C], k == 0, False))
+    need("p", t_c, k_t, t_ones)
+    p_b = run("p", p.matmul(T.pb_base[:, 0:K], T.tri[:], T.cnt[:], True, j == 0))
+    if j:
+        p.wait_ge(S.cn, EC * j)
+        for i in range(j):
+            p_b = run("p", p.matmul(T.pb_base[:, 0:K], T.ones[:, 0:128], T.cin[:, K * i:K * i + K], False, i == j - 1))
+    need("v", p_b)
+    for k in range(K):
+        t = run("v", v.tensor_scalar(T.ww[:, C * k:C * k + C], T.hot[:, C * k:C * k + C], T.pb_base[:, k:k + 1], None, MULT))
         need("p", t)
+        p_t = run("p", p.matmul(T.pb_pos[:, 0:C], T.ident[:], T.ww[:, C * k:C * k + C], False, k == K - 1))
+    need("v", p_t)
+    t_pos = run("v", v.tensor_copy(T.pos[:], T.pb_pos[:, 0:C]))
+    need("v", t_pos, k_a)
+    need("p", t_b)
+    for c in range(C):
+        t = run("v", v.tensor_scalar(T.oh_a[:, 256 * c:256 * c + 256], T.iota_a[:], T.pos[:, c:c + 1], None, EQ))
+        need("p", t, a_b[c])
         for b, xb in enumerate((T.pb_x0, T.pb_x1)):
-            p_x = run("p", p.matmul(xb[:, 0:32], T.oh_a[:, 256 * c + 128 * b:256 * c + 128 * b + 128],
-                                    T.oh_b[:, 32 * c:32 * c + 32], c == 0, c == C - 1))
+            p_x = run("p", p.matmul(xb[:, 0:64], T.oh_a[:, 256 * c + 128 * b:256 * c + 128 * b + 128],
+                                    T.oh_b[:, c::C], c == 0, c == C - 1))
     need("v", p_x)
     need("a", p_x)
     for kind in range(2):
-        t_x = run("v", v.tensor_copy(T.xs[:, 32 * kind:32 * kind + 16], T.pb_x0[:, 16 * kind:16 * kind + 16]))
-        a_x = run("a", a.activation(T.xs[:, 32 * kind + 16:32 * kind + 32], T.pb_x1[:, 16 * kind:16 * kind + 16], COPY))
+        run("v", v.tensor_copy(T.xs[:, 32 * kind:32 * kind + 16], T.pb_x0[:, 16 * kind:16 * kind + 16]))
+        run("a", a.activation(T.xs[:, 32 * kind + 16:32 * kind + 32], T.pb_x1[:, 16 * kind:16 * kind + 16], COPY))
+    t_x = run("v", v.tensor_copy(T.xt[:, 0:32], T.pb_x0[:, 32:64]))
+    a_x = run("a", a.activation(T.xt[:, 32:64], T.pb_x1[:, 32:64], COPY))
     need("g", t_x, a_x)
-    send(T.xs[:], T.xs_in[:, 64 * j:64 * j + 64], [d for d in (far, main) if d != core], S.x_s)
+    send([(T.xs[:], T.xs_in[:, 64 * j:64 * j + 64], others([far, main]), S.x_s, E),
+          (T.xt[:], T.xt_in[:, 64 * j:64 * j + 64], others(lay[:ND]), S.x_t, E, E)])
 
-    t_md, t_cd = counts("d")
-    inner("d")
-
-    def total_of(x_in, x_own, width, sem):
-        need("p", t_x, a_x)
-        p.wait_ge(sem, E * (NJ - 1))
-        for i in range(NJ):
-            src = x_own[:] if i == j else x_in[:, width * i:width * i + width]
-            t = run("p", p.matmul(T.pb_sum[:, 0:width], T.ident[:], src, i == 0, i == NJ - 1))
+    def total_of(parts, width, count, sem, *toks):
+        need("p", k_i, *toks)
+        p.wait_ge(sem, count)
+        for i, x in enumerate(parts):
+            t = run("p", p.matmul(T.pb_sum[:, 0:width], T.ident[:], x, i == 0, i == len(parts) - 1))
         return t
 
     if sender:
-        pt = total_of(T.xs_in, T.xs, 64, S.x_s)
+        pt = total_of([T.xs[:] if i == j else T.xs_in[:, 64 * i:64 * i + 64] for i in range(NJ)], 64, E * (NJ - 1), S.x_s,
+                      t_x, a_x)
         need("v", pt)
         t_t = run("v", v.tensor_copy(T.ts[:], T.pb_sum[:, 0:64]))
         need("p", t_t, k_lo, k_hi)
         for k in range(8):
-            run("p", p.matmul(T.pb_wrap[:, 32 * k:32 * k + 32], T.sel_lo[:, 128 * k:128 * k + 128], T.ts[:, 0:32], True, False))
-            pt = run("p", p.matmul(T.pb_wrap[:, 32 * k:32 * k + 32], T.sel_hi[:, 128 * k:128 * k + 128], T.ts[:, 32:64],
-                                   False, True))
+            o = T.pb_wrap[:, 32 * k:32 * k + 32]
+            run("p", p.matmul(o, T.sel_lo[:, 128 * k:128 * k + 128], T.ts[:, 0:32], True, False))
+            pt = run("p", p.matmul(o, T.sel_hi[:, 128 * k:128 * k + 128], T.ts[:, 32:64], False, True))
         need("v", pt)
         half = [x for x in range(N) if (x // 8 == rank // 8) == is_main]
         first = rank % 8 + 1
         peers = half[first:] + half[:first]
         for x in peers[0:2]:
             t = run("v", v.tensor_copy(T.off_s[:, 16 * x:16 * x + 16], T.pb_wrap[:, x:256:16]))
-        if is_main:
-            for q in (v, a):
+        for q in (v, a):
+            if is_main:
                 for i in range(NCH):
                     q.wait_ge(S["tl%d" % i], 16)
-        else:
-            v.wait_ge(S.tb, 16 * NCH)
-            a.wait_ge(S.tb, 16 * NCH)
+            else:
+                q.wait_ge(S.tb, 16 * NCH)
         toks = {}
         for i in range(0, 8, 2):
             for x, qn in ((peers[i], "v"), (peers[i + 1], "a")):
                 dst = T.win[:, R + CAPP * x:R + CAPP * x + CAPP] if x == rank else T.gat[:, CAPP * x:CAPP * x + CAPP]
                 src = T.win[:, 0:R].indirect(T.off_s[:, 16 * x:16 * x + 16])
                 need(qn, t)
-                if qn == "v":
-                    toks[x] = run("v", v.tensor_copy(dst, src))
-                else:
-                    toks[x] = run("a", a.activation(dst, src, COPY))
+                toks[x] = run("v", v.tensor_copy(dst, src)) if qn == "v" else run("a", a.activation(dst, src, COPY))
             for x in peers[i + 2:i + 4]:
                 t = run("v", v.tensor_copy(T.off_s[:, 16 * x:16 * x + 16], T.pb_wrap[:, x:256:16]))
         for i in range(0, 8, 4):
             grp = [x for x in peers[i:i + 4] if x != rank]
             need("g", *[toks[x] for x in grp])
-            tr = []
-            for i2, x in enumerate(grp):
-                d = T.cores[x]
-                tr.append(RemoteDMATransfer(dst_ids=[did(d)], dma_engine_mask=mask_to([d], 2, 2 * i2), remote_sem=S.arr,
-                                            srcs=[T.gat[:, CAPP * x:CAPP * x + CAPP]],
-                                            dsts=[T.win[:, R + CAPP * rank:R + CAPP * rank + CAPP]], alu_op=0))
-                loc[0] += 2
-            g.remote_dma_fused(tr, local_sem=S.loc)
+            send([(T.gat[:, CAPP * x:CAPP * x + CAPP], T.win[:, R + CAPP * rank:R + CAPP * rank + CAPP], [T.cores[x]], S.arr,
+                   2, 2 * i2) for i2, x in enumerate(grp)])
 
-    t1 = run("v", v.tensor_scalar(T.wi[:, 0:32], T.st[:, 32:64], 127, None, AluOpType.bitwise_and))
-    t2 = run("v", v.tensor_scalar(T.wi[:, 32:64], T.st[:, 32:64], 7, None, AluOpType.arith_shift_right))
-    need("v", t1, t2)
-    run("v", v.tensor_copy(T.wf[:, 0:64], T.wi[:]))
-    t1 = run("v", v.tensor_scalar(T.wf[:, 64:96], T.vv[:, 0:32], R // 256, None, ADD))
-    need("v", t1, k_l, k_b)
-    for c in range(C):
-        run("v", v.tensor_scalar(T.oh_l[:, 128 * c:128 * c + 128], T.iota_l[:], T.wf[:, c:c + 1], None, EQ))
-        t_hi = run("v", v.tensor_scalar(T.oh_c[:, 128 * c + 64:128 * c + 128], T.iota_b[:], T.wf[:, 32 + c:33 + c],
-                                        T.wf[:, 64 + c:65 + c], EQ, MULT))
-    t_pos = slots("d", t_cd)
-    need("v", t_pos)
-    need("p", t_x)
-    for c in range(C):
-        t = run("v", v.tensor_scalar(T.oh_c[:, 128 * c:128 * c + 64], T.iota_b[:], T.wf[:, 32 + c:33 + c],
-                                     T.pos_d[:, c:c + 1], EQ, MULT))
-        need("p", t)
-        p_x = run("p", p.matmul(T.pb_x0[:, 0:128], T.oh_l[:, 128 * c:128 * c + 128], T.oh_c[:, 128 * c:128 * c + 128],
-                                c == 0, c == C - 1))
-    need("v", p_x)
-    t_x = run("v", v.tensor_copy(T.xd[:], T.pb_x0[:, 0:128]))
-    if not is_main:
-        need("g", t_x)
-        send(T.xd[:], T.xd_in[:, 128 * j:128 * j + 128], [main], S.x_d)
+    if j < ND:
+        need("v", k_p, k_l, k_b)
+        t1 = run("v", v.tensor_scalar(T.pidx[:, 4:6], T.pidx[:, 0:2], 15, None, AN))
+        t2 = run("v", v.tensor_scalar(T.pidx[:, 6:8], T.pidx[:, 0:2], 4, None, SR))
+        need("v", t1, t2)
+        t = run("v", v.tensor_scalar(T.pidf[:, 2:4], T.pidx[:, 6:8], 32.0, 1.0, MULT, ADD))
+        need("v", t)
+        t1 = run("v", v.tensor_tensor(T.pidf[:, 0:1], T.pidf[:, 2:3], T.pidx[:, 4:5], ADD))
+        need("v", t1)
+        t_sl = run("v", v.tensor_scalar(T.pidf[:, 1:2], T.pidf[:, 0:1], 16.0, None, ADD))
+        pt = total_of([T.xt[:] if i == j else T.xt_in[:, 64 * i:64 * i + 64] for i in range(NJ)], 64, E * (NJ - 1), S.x_t,
+                      t_x, a_x)
+        need("v", pt)
+        need("a", pt)
+        for b in range(2):
+            at = 32 * b + 4 * j
+            t_dm = run("v", v.tensor_copy(T.dm[:, b::4], T.pb_sum[:, at:at + 4]))
+            a_dm = None
+        for b in range(2):
+            at = 32 * b + 16 + 4 * j
+            t_dm = run("v", v.tensor_copy(T.dm[:, 2 + b::4], T.pb_sum[:, at:at + 4]))
+        need("g", t_dm)
+        parts = []
+        for i in range(4):
+            d = layout(4 * j + i)[rank // 4]
+            if d != core:
+                parts.append((T.dm[:, 4 * i:4 * i + 4], T.din[:, 4 * (rank % 4):4 * (rank % 4) + 4], [d], S.dd, 2, 2 * i))
+        send(parts)
+        own = rank // 4 == j
+        need("v", t_sl, t_dm)
+        v.wait_ge(S.dd, 2 * (3 if own else 4))
+        for i in range(4):
+            src = T.dm[:, 4 * i:4 * i + 4] if 4 * j + i == rank else T.din[:, 4 * i:4 * i + 4]
+            t = run("v", v.tensor_copy(T.df[:, 4 * i:4 * i + 4], src))
+        need("v", t)
+        for i in range(4):
+            for b in range(2):
+                x = 2 * i + b
+                lo, hi = T.df[:, 4 * i + b:4 * i + b + 1], T.df[:, 4 * i + 2 + b:4 * i + 3 + b]
+                run("v", v.tensor_scalar(T.oh_l[:, 128 * x:128 * x + 128], T.iota_l[:], lo, None, EQ))
+                run("v", v.tensor_scalar(T.oh_c[:, 128 * x:128 * x + 64], T.iota_b[:], hi, T.pidf[:, b:b + 1], EQ, MULT))
+                t = run("v", v.tensor_scalar(T.oh_c[:, 128 * x + 64:128 * x + 128], T.iota_b[:], hi,
+                                             float(R // 256 + 4 * j + i), EQ, MULT))
+                need("p", t)
+                p_x = run("p", p.matmul(T.pb_wrap[:, 0:128], T.oh_l[:, 128 * x:128 * x + 128],
+                                        T.oh_c[:, 128 * x:128 * x + 128], x == 0, x == 7))
+        need("v", p_x)
+        t = run("v", v.tensor_copy(T.xd[:], T.pb_wrap[:, 0:128]))
+        need("g", t)
+        send([(T.xd[:], T.xd_in[:, 128 * j:128 * j + 128], [main], S.x_d, E)])
 
     if is_main:
         need("v", k_p, k_c)
-        t = run("v", v.tensor_scalar(T.pidx[:], T.pidx[:], 15, None, AluOpType.bitwise_and))
+        t = run("v", v.tensor_scalar(T.pidx[:], T.pidx[:], 15, None, AN))
         need("v", t)
         t = run("v", v.tensor_copy(T.pidf[:], T.pidx[:]))
         need("v", t)
         t_ic = run("v", v.tensor_scalar(T.iota_c[:], T.iota_c[:], T.pidf[:, 0:1], None, ADD))
-        need("p", t_t)
-        pt = total_of(T.xd_in, T.xd, 128, S.x_d)
+        pt = total_of([T.xd_in[:, 128 * i:128 * i + 128] for i in range(ND)], 128, E * ND, S.x_d, t_t)
         need("v", pt)
         t = run("v", v.tensor_copy(T.td[:], T.pb_sum[:, 0:128]))
         need("p", t)
         for k in range(8):
-            run("p", p.matmul(T.pb_wrap[:, 64 * k:64 * k + 64], T.sel_lo[:, 128 * k:128 * k + 128], T.td[:, 0:64], True, False))
-            pt = run("p", p.matmul(T.pb_wrap[:, 64 * k:64 * k + 64], T.sel_hi[:, 128 * k:128 * k + 128], T.td[:, 64:128],
-                                   False, True))
+            o = T.pb_wrap[:, 64 * k:64 * k + 64]
+            run("p", p.matmul(o, T.sel_lo[:, 128 * k:128 * k + 128], T.td[:, 0:64], True, False))
+            pt = run("p", p.matmul(o, T.sel_hi[:, 128 * k:128 * k + 128], T.td[:, 64:128], False, True))
         need("v", pt, t_ic)
         t = run("v", v.tensor_tensor(T.inv_f[:], T.pb_wrap[:], T.iota_c[:], MAX))
         need("v", t)
@@ -364,17 +370,18 @@ def rank_program(g, core, T, topo):
             t = run("v", v.tensor_scalar(T.off_d[:, k::8], T.inv_f[:, 64 * k:64 * k + 64], -1.0, None, ADD))
         v.wait_ge(S.arr, 2 * (N - 1))
         a.wait_ge(S.arr, 2 * (N - 1))
-        need("v", t, toks[peers[7]])
-        need("a", t, toks[peers[7]])
-        wy, ky = 1024, 64
-        ny = R // wy
-        for i in range(ny):
-            src = T.win[:].indirect(T.off_d[:, ky * i:ky * i + ky])
-            dst = T.out[:, wy * i:wy * i + wy]
-            t = run("v", v.tensor_copy(dst, src)) if i % 2 == 0 else run("a", a.activation(dst, src, COPY))
-            g.sync.wait_ge(S["q" + t[0]], t[1])
-            g.sync.dma_start(T.y[:, wy * i:wy * i + wy], dst).then_inc(S.ys, 16)
-        g.wait_ge(S.ys, 16 * ny)
+        need("v", t, toks[rank])
+        need("a", t, toks[rank])
+        at, n_y = 0, 0
+        for wy in Y_CHUNKS:
+            for qn in ("v", "a"):
+                src = T.win[:].indirect(T.off_d[:, at // 16:(at + wy) // 16])
+                dst = T.out[:, at:at + wy]
+                t = run("v", v.tensor_copy(dst, src)) if qn == "v" else run("a", a.activation(dst, src, COPY))
+                need("s", t)
+                g.sync.dma_start(T.y[:, at:at + wy], dst).then_inc(S.ys, 16)
+                at, n_y = at + wy, n_y + 1
+        g.wait_ge(S.ys, 16 * n_y)
 
     for q in ("v", "a", "p", "g"):
         if cnt[q]:

@@ -3,69 +3,81 @@ from concourse.mybir import AluOpType, ActivationFunctionType
 
 N, R, CAPP = 16, 8192, 256
 NJ, C, K = 8, 32, 16
+UP = 3
+KA = 11
 ND = 4
 NCH = 4
+W = R // NCH
 E, EC = 8, 16
-ADD, MULT, MAX, EQ = AluOpType.add, AluOpType.mult, AluOpType.max, AluOpType.is_equal
+ADD, SUB, MULT, EQ = AluOpType.add, AluOpType.subtract, AluOpType.mult, AluOpType.is_equal
 SR, AN = AluOpType.arith_shift_right, AluOpType.bitwise_and
-COPY = ActivationFunctionType.Copy
-Y_CHUNKS = (256, 768, 1024, 1024, 768, 256)
+COPY, ABS, RELU = ActivationFunctionType.Copy, ActivationFunctionType.Abs, ActivationFunctionType.Relu
+Y_CHUNKS = ((256, 256), (768, 768), (1024, 1024), (1024, 1024), (704, 832), (256, 256))
+GROUPS = ((0, 2, 4), (2, 4, 4), (4, 8, 2))
+Y1 = 128
 
 SCRATCH = {
     "lst": ("dram", [128, 32], "int32"),
     "lin": ("dram", [256, 32], "int32"),
     "st": ("sbuf", [128, 64], "int32"),
-    "uu": ("sbuf", [128, 32], "int32"),
-    "vv": ("sbuf", [128, 32], "int32"),
+    "uv": ("sbuf", [128, 64], "int32"),
     "key": ("sbuf", [128, 32], "float32"),
+    "kabs": ("sbuf", [128, 32 * (K - KA)], "float32"),
     "vi": ("sbuf", [128, 128], "int32"),
-    "vf": ("sbuf", [128, 128], "float32"),
+    "vb": ("sbuf", [128, 96], "bfloat16"),
+    "vf": ("sbuf", [128, 32], "float32"),
     "hot": ("sbuf", [128, 512], "bfloat16"),
     "inc": ("sbuf", [128, 512], "bfloat16"),
     "zz": ("sbuf", [128, 512], "bfloat16"),
     "ww": ("sbuf", [128, 512], "bfloat16"),
     "cnt": ("sbuf", [128, 16], "bfloat16"),
     "cin": ("sbuf", [128, 8 * 16], "bfloat16"),
-    "pos": ("sbuf", [128, 32], "float32"),
-    "ones": ("sbuf", [128, 1024], "bfloat16"),
-    "c256": ("sbuf", [128, 1024], "bfloat16"),
+    "pt": ("sbuf", [128, 32], "float32"),
+    "plo": ("sbuf", [128, 32], "float32"),
+    "psc": ("sbuf", [128, 32], "float32"),
+    "lin2": ("sbuf", [128, 2], "float32"),
+    "ones": ("sbuf", [128, 128], "bfloat16"),
+    "ends": ("sbuf", [128, 256], "bfloat16"),
     "ident": ("sbuf", [128, 128], "bfloat16"),
     "tri": ("sbuf", [128, 128], "bfloat16"),
     "rst": ("sbuf", [128, 512], "bfloat16"),
-    "iota_a": ("sbuf", [128, 256], "bfloat16"),
+    "iota_a": ("sbuf", [128, 128], "bfloat16"),
     "iota_l": ("sbuf", [128, 128], "bfloat16"),
     "iota_b": ("sbuf", [128, 64], "bfloat16"),
-    "iota_c": ("sbuf", [128, 512], "float32"),
-    "pidx": ("sbuf", [128, 8], "int32"),
-    "pidf": ("sbuf", [128, 8], "float32"),
-    "sel_lo": ("sbuf", [128, 1024], "bfloat16"),
-    "sel_hi": ("sbuf", [128, 1024], "bfloat16"),
-    "oh_a": ("sbuf", [128, 32 * 256], "bfloat16"),
-    "oh_b": ("sbuf", [128, 4 * 512], "bfloat16"),
+    "pc": ("sbuf", [128, 16], "float32"),
+    "cdef": ("sbuf", [128, 128], "bfloat16"),
+    "bsel": ("sbuf", [128, 128], "bfloat16"),
+    "grp": ("sbuf", [128, 128], "bfloat16"),
+    "grp128": ("sbuf", [128, 128], "bfloat16"),
+    "msk": ("sbuf", [128, 8], "float32"),
+    "oh_a": ("sbuf", [128, 32 * 128], "bfloat16"),
+    "oh_b": ("sbuf", [128, 64 * 32], "bfloat16"),
     "oh_l": ("sbuf", [128, 8 * 128], "bfloat16"),
+    "oh_m": ("sbuf", [128, 8 * 64], "bfloat16"),
     "oh_c": ("sbuf", [128, 8 * 128], "bfloat16"),
-    "xs": ("sbuf", [128, 64], "bfloat16"),
-    "xt": ("sbuf", [128, 64], "bfloat16"),
-    "xs_in": ("sbuf", [128, 8 * 64], "bfloat16"),
-    "xt_in": ("sbuf", [128, 8 * 64], "bfloat16"),
+    "xi": ("sbuf", [128, 64], "int32"),
+    "xlh": ("sbuf", [128, 128], "int32"),
+    "xa": ("sbuf", [128, 128], "bfloat16"),
+    "xin": ("sbuf", [128, 8 * 128], "bfloat16"),
     "dm": ("sbuf", [128, 16], "bfloat16"),
-    "din": ("sbuf", [128, 16], "bfloat16"),
-    "df": ("sbuf", [128, 16], "float32"),
+    "din": ("sbuf", [128, 64], "bfloat16"),
+    "duw": ("sbuf", [128, 16], "float32"),
     "xd": ("sbuf", [128, 128], "bfloat16"),
     "xd_in": ("sbuf", [128, 4 * 128], "bfloat16"),
-    "ts": ("sbuf", [128, 64], "bfloat16"),
-    "td": ("sbuf", [128, 128], "bfloat16"),
-    "off_s": ("sbuf", [128, 256], "uint16"),
-    "inv_f": ("sbuf", [128, 512], "float32"),
+    "ts": ("sbuf", [128, 32], "bfloat16"),
+    "rw": ("sbuf", [128, 256], "bfloat16"),
+    "ru": ("sbuf", [128, 512], "bfloat16"),
+    "rv": ("sbuf", [128, 512], "bfloat16"),
+    "off_s": ("sbuf", [128, 128], "uint16"),
     "off_d": ("sbuf", [128, 512], "uint16"),
     "win": ("sbuf", [128, R + N * CAPP], "bfloat16"),
     "gat": ("sbuf", [128, N * CAPP], "bfloat16"),
     "out": ("sbuf", [128, R], "bfloat16"),
 }
-for _b in ("pb_base", "pb_pos", "pb_x0", "pb_x1", "pb_sum", "pb_wrap"):
+for _b in ("pb_base", "pb_pos", "pb_x", "pb_hot", "pb_vf", "pb_sum", "pb_wrap"):
     SCRATCH[_b] = ("psum", [128, 512], "float32")
 
-SEMAPHORES = ["qv", "qa", "qp", "qg", "lcopy", "lsent", "la0", "la1", "ld", "loc", "cn", "x_s", "x_t", "dd", "x_d", "tb",
+SEMAPHORES = ["qv", "qa", "qp", "qg", "lcopy", "lsent", "la0", "la1", "ld", "loc", "cn", "x_s", "dd", "x_d", "tb",
               "arr", "ys", "tl0", "tl1", "tl2", "tl3"]
 
 
@@ -113,6 +125,10 @@ def rank_program(g, core, T, topo):
                 Q[q].wait_ge(S["q" + s], n)
                 seen[(q, s)] = n
 
+    def place(x, d):
+        at = (d - x - 1) % 8
+        return [i for i, y in enumerate(GROUPS) if y[0] <= at < y[1]][0]
+
     def did(d):
         rid, pid = topo.addr(d, core)
         return DstId(rid=rid, pnc=pid)
@@ -137,26 +153,63 @@ def rank_program(g, core, T, topo):
     def others(cs):
         return [c for c in cs if c != core]
 
+    def iota(out, pattern, base, cm):
+        return run("g", g.iota(out, pattern, base, cm, allow_small_or_imprecise_dtypes=True))
+
+    def load_tab(i):
+        g.sync.dma_start(T.win[:, W * i:W * i + W], T.tab[:, W * i:W * i + W]).then_inc(S["tl%d" % i], 16)
+
     if is_main:
         g.sync.dma_start(T.lst[0:64, :], T.src[:]).then_inc(S.lcopy, 16)
         g.scalar.dma_start(T.lst[64:128, :], T.dst[:]).then_inc(S.lcopy, 16)
+        load_tab(0)
     t_ones = run("v", v.memset(T.ones[:], 1.0))
-    k_a = run("g", g.iota(T.iota_a[:], [[16, 2], [32, 8], [1, 16]], 1, 0, allow_small_or_imprecise_dtypes=True))
+    t_r = run("v", v.memset(T.rst[:], 1.0))
+    need("v", t_r)
+    t_r = run("v", v.memset(T.rst[:, 0::C], 0.0))
+    if sender:
+        t_k = run("v", v.memset(T.msk[:], 1.0))
+    ends = [(slice(0, 64), True), (slice(64, 128), False)] if is_main else [(slice(0, 128), j < UP)]
+    for rows, up in ends:
+        run("v", v.memset(T.lin2[rows, 0:1], 255.0 / 128.0 if up else -255.0 / 128.0))
+        run("v", v.memset(T.lin2[rows, 1:2], 1.0 if up else 256.0))
+        k_a = iota(T.iota_a[rows, :], [[1 if up else -1, 128]], 1 if up else 128, 0)
+        if is_main:
+            need("g", k_a)
+    if is_main:
+        run("v", v.memset(T.ends[:, 0:64], 1.0))
+        run("v", v.memset(T.ends[:, 64:192], 0.0))
+        t_ones = run("v", v.memset(T.ends[:, 192:256], 1.0))
     need("g", t_ones)
-    k_i = run("g", g.affine_select(T.ident[:], T.ones[:, 0:128], [[-1, 128]], EQ, 0.0, 0, 1))
+    k_i = run("g", g.affine_select(T.ident[:], T.ones[:], [[-1, 128]], EQ, 0.0, 0, 1))
     if is_main:
         k = rank % 2
-        dsts = others([layout(h)[rank // 2] for h in range(N)])
+        dsts = others([layout((rank + 1 + h) % N)[rank // 2] for h in range(N)])
         g.wait_ge(S.lcopy, 32)
         send([(T.lst[:], T.lin[128 * k:128 * k + 128, :], dsts, S["la%d" % k], E)], S.lsent)
-    k_t = run("g", g.affine_select(T.tri[:], T.ones[:, 0:128], [[1, 128]], AluOpType.is_gt, 0.0, 0, -1))
-    k_r = run("g", g.affine_select(T.rst[:], T.ones[:, 0:512], [[0, K], [1, C]], AluOpType.not_equal, 0.0, 0, 0))
-    if j < ND:
-        k_l = run("g", g.iota(T.iota_l[:], [[1, 128]], 0, 0, allow_small_or_imprecise_dtypes=True))
-        k_b = run("g", g.iota(T.iota_b[:], [[1, 64]], 1, 0, allow_small_or_imprecise_dtypes=True))
-        k_p = run("g", g.iota(T.pidx[:], [[0, 8]], 0, 1))
+    k_t = run("g", g.affine_select(T.tri[:], T.ones[:], [[1, 128]], AluOpType.is_gt, 0.0, 0, -1))
+    if is_main:
+        need("v", k_t)
+        k_t = run("v", v.memset(T.tri[0:64, 64:128], 0.0))
     if sender:
-        t_256 = run("v", v.memset(T.c256[:], 256.0))
+        k_s = run("g", g.affine_select(T.bsel[:], T.ones[:], [[0, 8], [-1, 16]], EQ, 0.0, 0, 1))
+        need("g", t_k)
+        k_m = run("g", g.affine_select(T.msk[:], T.msk[:], [[-16, 8]], AluOpType.is_ge, 0.0, 0, 1))
+        need("g", k_m)
+        k_m = run("g", g.affine_select(T.msk[:], T.msk[:], [[16, 8]], AluOpType.is_ge, 0.0, 15, -1))
+        need("p", k_s)
+        pt = run("p", p.matmul(T.pb_wrap[:, 0:128], T.bsel[:], T.bsel[:], True, True))
+        need("v", pt)
+        run("v", v.tensor_copy(T.grp[:], T.pb_wrap[:, 0:128]))
+        t_g = run("v", v.tensor_scalar(T.grp128[:], T.pb_wrap[:, 0:128], 128.0, None, MULT))
+    if is_main:
+        iota(T.cdef[:, 0:64], [[0, 64]], 0, 1)
+        k_c = iota(T.cdef[:, 64:128], [[1, 64]], 0, 0)
+    if j < ND:
+        iota(T.iota_l[:], [[1, 128]], 0, 0)
+        iota(T.iota_b[:], [[1, 64]], 1, 0)
+        iota(T.pc[:, 8:16], [[1, 8]], R // 128 + 1 + 8 * j, 0)
+        k_p = iota(T.pc[:, 0:8], [[0, 8]], 0, 1)
     for k in range(2):
         q = g.sync if k == 0 or is_main else g.scalar
         if is_main and rank == 2 * j + k:
@@ -167,115 +220,138 @@ def rank_program(g, core, T, topo):
         q.dma_start(T.st[64 * k:64 * k + 64, 0:32], s_in).then_inc(S.ld, 16)
         q.dma_start(T.st[64 * k:64 * k + 64, 32:64], d_in).then_inc(S.ld, 16)
     if is_main:
-        w = R // NCH
         g.sync.wait_ge(S.lsent, E)
-        for i in range(NCH):
-            g.sync.dma_start(T.win[:, w * i:w * i + w], T.tab[:, w * i:w * i + w]).then_inc(S["tl%d" % i], 16)
+        for i in range(1, NCH):
+            load_tab(i)
         for i in range(NCH):
             g.wait_ge(S["tl%d" % i], 16)
-            send([(T.win[:, w * i:w * i + w], T.win[:, w * i:w * i + w], [far], S.tb, 16)])
-    if sender:
-        pat = [[-16, 8], [0, 8], [-1, 16]]
-        k_lo = run("g", g.affine_select(T.sel_lo[:], T.ones[:], pat, EQ, 0.0, 0, 1))
-        need("g", t_256)
-        k_hi = run("g", g.affine_select(T.sel_hi[:], T.c256[:], pat, EQ, 0.0, 0, 1))
-    if is_main:
-        k_p = run("g", g.iota(T.pidx[:], [[0, 8]], 0, 1))
-        k_c = run("g", g.iota(T.iota_c[:], [[16, 8], [128, 64]], 1, 0, allow_small_or_imprecise_dtypes=True))
+            send([(T.win[:, W * i:W * i + W], T.win[:, W * i:W * i + W], [far], S.tb, 16)])
 
     v.wait_ge(S.ld, 64)
-    t1 = run("v", v.tensor_scalar(T.uu[:], T.st[:, 0:32], 8, 480, SR, AN))
-    t2 = run("v", v.tensor_scalar(T.vv[:], T.st[:, 32:64], 13, None, SR))
+    t1 = run("v", v.tensor_scalar(T.uv[:, 0:32], T.st[:, 0:32], 8, 480, SR, AN))
+    t2 = run("v", v.tensor_scalar(T.uv[:, 32:64], T.st[:, 32:64], 13, None, SR))
     need("v", t1, t2)
-    t = run("v", v.tensor_tensor(T.key[:], T.uu[:], T.vv[:], ADD))
+    t = run("v", v.tensor_tensor(T.key[:], T.uv[:, 0:32], T.uv[:, 32:64], ADD))
     need("v", t)
-    for k in range(K):
+    need("a", t)
+    for k in range(KA):
         t_m = run("v", v.tensor_scalar(T.hot[:, C * k:C * k + C], T.key[:], float(32 * rank + k), None, EQ))
-    need("v", t_m, k_r)
+    for k in range(KA, K):
+        t = run("a", a.activation(T.kabs[:, C * (k - KA):C * (k - KA) + C], T.key[:], ABS, bias=-float(32 * rank + k)))
+    need("a", t)
+    a_m = run("a", a.activation(T.hot[:, C * KA:C * K], T.kabs[:], RELU, bias=1.0, scale=-1.0))
+    need("v", t_m, a_m, t_r)
     t_q = run("v", v.tensor_tensor_scan(T.inc[:], T.rst[:], T.hot[:], 0.0, MULT, ADD))
     need("v", t_q)
     t_c = run("v", v.tensor_copy(T.cnt[:], T.inc[:, C - 1::C]))
     if j < last:
         need("g", t_c)
-        send([(T.cnt[:], T.cin[:, K * j:K * j + K], lay[j + 1:], S.cn, EC)])
-    run("v", v.tensor_scalar(T.vi[:, 0:32], T.st[:, 0:32], 255, None, AN))
-    run("v", v.tensor_scalar(T.vi[:, 32:64], T.st[:, 0:32], 8, 31, SR, AN))
-    run("v", v.tensor_scalar(T.vi[:, 64:96], T.st[:, 32:64], 127, None, AN))
-    t1 = run("v", v.tensor_scalar(T.vi[:, 96:128], T.st[:, 32:64], 7, 63, SR, AN))
+        send([(T.cnt[:], T.cin[:, K * j:K * j + K], (lay[j + 1:UP] if j < UP else lay[j + 1:last]) + [main], S.cn, EC)])
+    need("p", t_m, a_m, k_i)
+    p_h = run("p", p.matmul(T.pb_hot[:], T.ident[:], T.hot[:], True, True))
+    t = run("v", v.tensor_scalar(T.vi[:, 96:128], T.st[:, 32:64], 7, 63, SR, AN))
+    run("v", v.tensor_scalar(T.vi[:, 0:32], T.st[:, 0:32], 127, None, AN))
+    run("v", v.tensor_scalar(T.vi[:, 32:64], T.st[:, 0:32], 7, 63, SR, AN))
+    t1 = run("v", v.tensor_scalar(T.vi[:, 64:96], T.st[:, 32:64], 127, None, AN))
+    need("v", t)
+    t_vf = run("v", v.tensor_scalar(T.vf[:], T.vi[:, 96:128], 1.0, None, ADD))
     need("v", t1)
-    run("v", v.tensor_copy(T.vf[:, 0:96], T.vi[:, 0:96]))
-    t_vf = run("v", v.tensor_scalar(T.vf[:, 96:128], T.vi[:, 96:128], 1.0, None, ADD))
-    need("a", t_vf, t_m)
+    t_vb = run("v", v.tensor_copy(T.vb[:], T.vi[:, 0:96]))
+    need("a", t_vf, t_m, a_m)
     a_b = []
     for c in range(C):
-        for kind in (2, 3):
-            t = run("a", a.activation(T.oh_b[:, 512 * kind + c:512 * kind + 512:C], T.hot[:, c::C], COPY,
-                                      scale=T.vf[:, 32 * kind + c:32 * kind + c + 1]))
-        a_b.append(t)
-    t_z = run("v", v.tensor_tensor(T.zz[:], T.inc[:], T.hot[:], MULT))
-    need("v", t_vf)
-    for kind in (0, 1):
-        for k in range(K):
-            t_b = run("v", v.tensor_tensor(T.oh_b[:, 512 * kind + C * k:512 * kind + C * k + C], T.hot[:, C * k:C * k + C],
-                                           T.vf[:, 32 * kind:32 * kind + 32], MULT))
-    need("p", t_z, k_i)
+        a_b.append(run("a", a.activation(T.oh_b[:, C * 48 + c:C * 64:C], T.hot[:, c::C], COPY, scale=T.vf[:, c:c + 1])))
+    need("p", t_vb)
+    for kind in range(3):
+        for i in range(2):
+            p_v = run("p", p.matmul(T.pb_vf[:, 64 * kind + 32 * i:64 * kind + 32 * i + 32], T.ident[:],
+                                    T.vb[:, 32 * kind:32 * kind + 32], True, True))
+    need("v", p_h)
+    t_z = run("v", v.tensor_tensor(T.zz[:], T.inc[:], T.pb_hot[:], MULT))
+    need("v", p_v)
+    for kind in range(3):
+        for k in range(0, K, 2):
+            row = 16 * (k // 8) + 8 * kind + k % 8 if kind < 2 else 32 + k
+            t_b = run("v", v.tensor_tensor(T.oh_b[:, C * row:C * row + 2 * C], T.hot[:, C * k:C * k + 2 * C],
+                                           T.pb_vf[:, 64 * kind:64 * kind + 64], MULT))
+    need("p", t_z)
     for k in range(K):
         run("p", p.matmul(T.pb_pos[:, 0:C], T.ident[:], T.zz[:, C * k:C * k + C], k == 0, False))
+    before = list(range(last)) if is_main else list(range(j)) if j < UP else list(range(UP, j))
     need("p", t_c, k_t, t_ones)
-    p_b = run("p", p.matmul(T.pb_base[:, 0:K], T.tri[:], T.cnt[:], True, j == 0))
-    if j:
-        p.wait_ge(S.cn, EC * j)
-        for i in range(j):
-            p_b = run("p", p.matmul(T.pb_base[:, 0:K], T.ones[:, 0:128], T.cin[:, K * i:K * i + K], False, i == j - 1))
+    p_b = run("p", p.matmul(T.pb_base[:, 0:K], T.tri[:], T.cnt[:], True, not before))
+    if before:
+        p.wait_ge(S.cn, EC * len(before))
+        for i in before:
+            lhs = T.ones[:] if not is_main else T.ends[:, 0:128] if i < UP else T.ends[:, 128:256]
+            p_b = run("p", p.matmul(T.pb_base[:, 0:K], lhs, T.cin[:, K * i:K * i + K], False, i == before[-1]))
     need("v", p_b)
     for k in range(K):
         t = run("v", v.tensor_scalar(T.ww[:, C * k:C * k + C], T.hot[:, C * k:C * k + C], T.pb_base[:, k:k + 1], None, MULT))
         need("p", t)
         p_t = run("p", p.matmul(T.pb_pos[:, 0:C], T.ident[:], T.ww[:, C * k:C * k + C], False, k == K - 1))
     need("v", p_t)
-    t_pos = run("v", v.tensor_copy(T.pos[:], T.pb_pos[:, 0:C]))
+    t = run("v", v.tensor_scalar(T.pt[:], T.pb_pos[:, 0:C], 128.0, 128.0, AluOpType.is_gt, MULT))
+    need("v", t)
+    run("v", v.tensor_tensor(T.plo[:], T.pb_pos[:, 0:C], T.pt[:], SUB))
+    t_pos = run("v", v.tensor_scalar(T.psc[:], T.pt[:], T.lin2[:, 0:1], T.lin2[:, 1:2], MULT, ADD))
     need("v", t_pos, k_a)
     need("p", t_b)
     for c in range(C):
-        t = run("v", v.tensor_scalar(T.oh_a[:, 256 * c:256 * c + 256], T.iota_a[:], T.pos[:, c:c + 1], None, EQ))
+        t = run("v", v.tensor_scalar(T.oh_a[:, 128 * c:128 * c + 128], T.iota_a[:], T.plo[:, c:c + 1], T.psc[:, c:c + 1],
+                                     EQ, MULT))
         need("p", t, a_b[c])
-        for b, xb in enumerate((T.pb_x0, T.pb_x1)):
-            p_x = run("p", p.matmul(xb[:, 0:64], T.oh_a[:, 256 * c + 128 * b:256 * c + 128 * b + 128],
-                                    T.oh_b[:, c::C], c == 0, c == C - 1))
+        p_x = run("p", p.matmul(T.pb_x[:, 0:64], T.oh_a[:, 128 * c:128 * c + 128], T.oh_b[:, c::C], c == 0, c == C - 1))
     need("v", p_x)
-    need("a", p_x)
-    for kind in range(2):
-        run("v", v.tensor_copy(T.xs[:, 32 * kind:32 * kind + 16], T.pb_x0[:, 16 * kind:16 * kind + 16]))
-        run("a", a.activation(T.xs[:, 32 * kind + 16:32 * kind + 32], T.pb_x1[:, 16 * kind:16 * kind + 16], COPY))
-    t_x = run("v", v.tensor_copy(T.xt[:, 0:32], T.pb_x0[:, 32:64]))
-    a_x = run("a", a.activation(T.xt[:, 32:64], T.pb_x1[:, 32:64], COPY))
-    need("g", t_x, a_x)
-    send([(T.xs[:], T.xs_in[:, 64 * j:64 * j + 64], others([far, main]), S.x_s, E),
-          (T.xt[:], T.xt_in[:, 64 * j:64 * j + 64], others(lay[:ND]), S.x_t, E, E)])
+    t = run("v", v.tensor_copy(T.xi[:], T.pb_x[:, 0:64]))
+    need("v", t)
+    t1 = run("v", v.tensor_scalar(T.xlh[:, 0:64], T.xi[:], 255, None, AN))
+    t2 = run("v", v.tensor_scalar(T.xlh[:, 64:128], T.xi[:], 8, None, SR))
+    need("v", t1)
+    run("v", v.tensor_copy(T.xa[:, 0::2], T.xlh[:, 0:64]))
+    need("v", t2)
+    t_x = run("v", v.tensor_copy(T.xa[:, 1::2], T.xlh[:, 64:128]))
+    need("g", t_x)
+    send([(T.xa[:], T.xin[:, 128 * j:128 * j + 128], others([main, far] + lay[:ND]), S.x_s, EC)])
 
-    def total_of(parts, width, count, sem, *toks):
-        need("p", k_i, *toks)
-        p.wait_ge(sem, count)
+    def total(o, parts):
         for i, x in enumerate(parts):
-            t = run("p", p.matmul(T.pb_sum[:, 0:width], T.ident[:], x, i == 0, i == len(parts) - 1))
+            t = run("p", p.matmul(o, T.ident[:], x, i == 0, i == len(parts) - 1))
         return t
 
     if sender:
-        pt = total_of([T.xs[:] if i == j else T.xs_in[:, 64 * i:64 * i + 64] for i in range(NJ)], 64, E * (NJ - 1), S.x_s,
-                      t_x, a_x)
+        hf = rank // 8 if is_main else 1 - rank // 8
+        need("p", t_x)
+        p.wait_ge(S.x_s, EC * (NJ - 1))
+        pt = total(T.pb_sum[:, 0:32], [T.xa[:, 32 * hf:32 * hf + 32] if i == j else
+                                       T.xin[:, 128 * i + 32 * hf:128 * i + 32 * hf + 32] for i in range(NJ)])
+        need("v", pt, k_m)
+        t_t = run("v", v.tensor_copy(T.ts[:], T.pb_sum[:, 0:32]))
+        need("v", t_t)
+        need("a", t_t, k_m)
+        for k in range(0, 8, 2):
+            t1 = run("v", v.tensor_scalar(T.rw[:, k::8], T.ts[:], T.msk[:, k:k + 1], None, MULT))
+            a1 = run("a", a.activation(T.rw[:, k + 1::8], T.ts[:], COPY, scale=T.msk[:, k + 1:k + 2]))
+        need("p", t1, a1, t_g)
+        run("p", p.matmul(T.pb_wrap[:, 0:128], T.grp[:], T.rw[:, 0:128], True, False))
+        pt = run("p", p.matmul(T.pb_wrap[:, 0:128], T.grp128[:], T.rw[:, 128:256], False, True))
         need("v", pt)
-        t_t = run("v", v.tensor_copy(T.ts[:], T.pb_sum[:, 0:64]))
-        need("p", t_t, k_lo, k_hi)
-        for k in range(8):
-            o = T.pb_wrap[:, 32 * k:32 * k + 32]
-            run("p", p.matmul(o, T.sel_lo[:, 128 * k:128 * k + 128], T.ts[:, 0:32], True, False))
-            pt = run("p", p.matmul(o, T.sel_hi[:, 128 * k:128 * k + 128], T.ts[:, 32:64], False, True))
-        need("v", pt)
-        half = [x for x in range(N) if (x // 8 == rank // 8) == is_main]
+        half = list(range(8 * hf, 8 * hf + 8))
         first = rank % 8 + 1
         peers = half[first:] + half[:first]
-        for x in peers[0:2]:
-            t = run("v", v.tensor_copy(T.off_s[:, 16 * x:16 * x + 16], T.pb_wrap[:, x:256:16]))
+
+        def offsets(xs):
+            xs = sorted(x % 8 for x in xs)
+            while xs:
+                n = 1
+                while n < len(xs) and xs[n] == xs[0] + n:
+                    n += 1
+                at = 16 * xs[0]
+                t = run("v", v.tensor_copy(T.off_s[:, at:at + 16 * n], T.pb_wrap[:, at:at + 16 * n]))
+                xs = xs[n:]
+            return t
+
+        t = offsets(peers[0:2])
         for q in (v, a):
             if is_main:
                 for i in range(NCH):
@@ -286,61 +362,53 @@ def rank_program(g, core, T, topo):
         for i in range(0, 8, 2):
             for x, qn in ((peers[i], "v"), (peers[i + 1], "a")):
                 dst = T.win[:, R + CAPP * x:R + CAPP * x + CAPP] if x == rank else T.gat[:, CAPP * x:CAPP * x + CAPP]
-                src = T.win[:, 0:R].indirect(T.off_s[:, 16 * x:16 * x + 16])
+                src = T.win[:, 0:R].indirect(T.off_s[:, 16 * (x % 8):16 * (x % 8) + 16])
                 need(qn, t)
                 toks[x] = run("v", v.tensor_copy(dst, src)) if qn == "v" else run("a", a.activation(dst, src, COPY))
-            for x in peers[i + 2:i + 4]:
-                t = run("v", v.tensor_copy(T.off_s[:, 16 * x:16 * x + 16], T.pb_wrap[:, x:256:16]))
-        for i in range(0, 8, 4):
-            grp = [x for x in peers[i:i + 4] if x != rank]
+            if i == 0:
+                t = offsets(peers[2:])
+        for i0, i1, n in GROUPS:
+            grp = [x for x in peers[i0:i1] if x != rank]
             need("g", *[toks[x] for x in grp])
             send([(T.gat[:, CAPP * x:CAPP * x + CAPP], T.win[:, R + CAPP * rank:R + CAPP * rank + CAPP], [T.cores[x]], S.arr,
-                   2, 2 * i2) for i2, x in enumerate(grp)])
+                   n, n * i2) for i2, x in enumerate(grp)])
 
     if j < ND:
-        need("v", k_p, k_l, k_b)
-        t1 = run("v", v.tensor_scalar(T.pidx[:, 4:6], T.pidx[:, 0:2], 15, None, AN))
-        t2 = run("v", v.tensor_scalar(T.pidx[:, 6:8], T.pidx[:, 0:2], 4, None, SR))
-        need("v", t1, t2)
-        t = run("v", v.tensor_scalar(T.pidf[:, 2:4], T.pidx[:, 6:8], 32.0, 1.0, MULT, ADD))
-        need("v", t)
-        t1 = run("v", v.tensor_tensor(T.pidf[:, 0:1], T.pidf[:, 2:3], T.pidx[:, 4:5], ADD))
-        need("v", t1)
-        t_sl = run("v", v.tensor_scalar(T.pidf[:, 1:2], T.pidf[:, 0:1], 16.0, None, ADD))
-        pt = total_of([T.xt[:] if i == j else T.xt_in[:, 64 * i:64 * i + 64] for i in range(NJ)], 64, E * (NJ - 1), S.x_t,
-                      t_x, a_x)
+        need("p", t_x)
+        p.wait_ge(S.x_s, EC * (NJ - 1))
+        pt = total(T.pb_sum[:, 0:64], [T.xa[:, 64:128] if i == j else T.xin[:, 128 * i + 64:128 * i + 128] for i in range(NJ)])
         need("v", pt)
-        need("a", pt)
-        for b in range(2):
-            at = 32 * b + 4 * j
-            t_dm = run("v", v.tensor_copy(T.dm[:, b::4], T.pb_sum[:, at:at + 4]))
-            a_dm = None
-        for b in range(2):
-            at = 32 * b + 16 + 4 * j
-            t_dm = run("v", v.tensor_copy(T.dm[:, 2 + b::4], T.pb_sum[:, at:at + 4]))
+        run("v", v.tensor_copy(T.dm[:, 0:8], T.pb_sum[:, 8 * j:8 * j + 8]))
+        t_dm = run("v", v.tensor_copy(T.dm[:, 8:16], T.pb_sum[:, 32 + 8 * j:40 + 8 * j]))
         need("g", t_dm)
+        me = rank % 4
         parts = []
         for i in range(4):
             d = layout(4 * j + i)[rank // 4]
             if d != core:
-                parts.append((T.dm[:, 4 * i:4 * i + 4], T.din[:, 4 * (rank % 4):4 * (rank % 4) + 4], [d], S.dd, 2, 2 * i))
+                parts.append((T.dm[:], T.din[:, 16 * me:16 * me + 16], [d], S.dd, 2, 2 * i))
         send(parts)
         own = rank // 4 == j
-        need("v", t_sl, t_dm)
+        need("v", t_dm, k_p)
+        if own:
+            t = run("v", v.tensor_copy(T.din[:, 16 * me:16 * me + 16], T.dm[:]))
+            need("v", t)
         v.wait_ge(S.dd, 2 * (3 if own else 4))
-        for i in range(4):
-            src = T.dm[:, 4 * i:4 * i + 4] if 4 * j + i == rank else T.din[:, 4 * i:4 * i + 4]
-            t = run("v", v.tensor_copy(T.df[:, 4 * i:4 * i + 4], src))
-        need("v", t)
+        for b in range(2):
+            run("v", v.tensor_scalar(T.duw[:, b:8:2], T.din[:, 2 * me + b::16], -1.0, T.pc[:, 0:1], MULT, ADD))
+            t_d = run("v", v.tensor_tensor(T.duw[:, 8 + b::2], T.pc[:, 8 + b::2], T.din[:, 8 + 2 * me + b::16], SUB))
+        need("a", t_d)
         for i in range(4):
             for b in range(2):
-                x = 2 * i + b
-                lo, hi = T.df[:, 4 * i + b:4 * i + b + 1], T.df[:, 4 * i + 2 + b:4 * i + 3 + b]
-                run("v", v.tensor_scalar(T.oh_l[:, 128 * x:128 * x + 128], T.iota_l[:], lo, None, EQ))
-                run("v", v.tensor_scalar(T.oh_c[:, 128 * x:128 * x + 64], T.iota_b[:], hi, T.pidf[:, b:b + 1], EQ, MULT))
-                t = run("v", v.tensor_scalar(T.oh_c[:, 128 * x + 64:128 * x + 128], T.iota_b[:], hi,
-                                             float(R // 256 + 4 * j + i), EQ, MULT))
-                need("p", t)
+                x, at = 2 * i + b, 16 * i + 2 * me + b
+                t = run("v", v.tensor_scalar(T.oh_m[:, 64 * x:64 * x + 64], T.iota_b[:], T.din[:, at + 8:at + 9], None, EQ))
+                t1 = run("v", v.tensor_scalar(T.oh_l[:, 128 * x:128 * x + 128], T.iota_l[:], T.din[:, at:at + 1], None, EQ))
+                need("a", t)
+                run("a", a.activation(T.oh_c[:, 128 * x:128 * x + 64], T.oh_m[:, 64 * x:64 * x + 64], COPY,
+                                      scale=T.duw[:, x:x + 1]))
+                a1 = run("a", a.activation(T.oh_c[:, 128 * x + 64:128 * x + 128], T.oh_m[:, 64 * x:64 * x + 64], COPY,
+                                           scale=T.duw[:, 8 + x:9 + x]))
+                need("p", t1, a1)
                 p_x = run("p", p.matmul(T.pb_wrap[:, 0:128], T.oh_l[:, 128 * x:128 * x + 128],
                                         T.oh_c[:, 128 * x:128 * x + 128], x == 0, x == 7))
         need("v", p_x)
@@ -349,34 +417,40 @@ def rank_program(g, core, T, topo):
         send([(T.xd[:], T.xd_in[:, 128 * j:128 * j + 128], [main], S.x_d, E)])
 
     if is_main:
-        need("v", k_p, k_c)
-        t = run("v", v.tensor_scalar(T.pidx[:], T.pidx[:], 15, None, AN))
-        need("v", t)
-        t = run("v", v.tensor_copy(T.pidf[:], T.pidx[:]))
-        need("v", t)
-        t_ic = run("v", v.tensor_scalar(T.iota_c[:], T.iota_c[:], T.pidf[:, 0:1], None, ADD))
-        pt = total_of([T.xd_in[:, 128 * i:128 * i + 128] for i in range(ND)], 128, E * ND, S.x_d, t_t)
-        need("v", pt)
-        t = run("v", v.tensor_copy(T.td[:], T.pb_sum[:, 0:128]))
-        need("p", t)
+        need("p", k_c, t_t)
+        p.wait_ge(S.x_d, E * ND)
+        p_u, p_w = [total(o[:, 0:64], [T.xd_in[:, 128 * i + h:128 * i + h + 64] for i in range(ND)] + [T.cdef[:, h:h + 64]])
+                    for o, h in ((T.pb_sum, 0), (T.pb_pos, 64))]
+        need("v", p_u)
+        need("a", p_w)
         for k in range(8):
-            o = T.pb_wrap[:, 64 * k:64 * k + 64]
-            run("p", p.matmul(o, T.sel_lo[:, 128 * k:128 * k + 128], T.td[:, 0:64], True, False))
-            pt = run("p", p.matmul(o, T.sel_hi[:, 128 * k:128 * k + 128], T.td[:, 64:128], False, True))
-        need("v", pt, t_ic)
-        t = run("v", v.tensor_tensor(T.inv_f[:], T.pb_wrap[:], T.iota_c[:], MAX))
-        need("v", t)
-        for k in range(8):
-            t = run("v", v.tensor_scalar(T.off_d[:, k::8], T.inv_f[:, 64 * k:64 * k + 64], -1.0, None, ADD))
-        v.wait_ge(S.arr, 2 * (N - 1))
-        a.wait_ge(S.arr, 2 * (N - 1))
-        need("v", t, toks[rank])
-        need("a", t, toks[rank])
+            t_u = run("v", v.tensor_scalar(T.ru[:, k::8], T.pb_sum[:, 0:64], T.msk[:, k:k + 1], None, MULT))
+            a_w = run("a", a.activation(T.rv[:, k::8], T.pb_pos[:, 0:64], COPY, scale=T.msk[:, k:k + 1]))
+        need("p", t_u, a_w)
+        t_o, offs = [], ((T.pb_x, 0, Y1), (T.pb_hot, Y1, R // 16))
+        for o, lo, hi in offs:
+            run("p", p.matmul(o[:, 0:hi - lo], T.grp[:], T.ru[:, lo:hi], True, False))
+            t_o.append(run("p", p.matmul(o[:, 0:hi - lo], T.grp128[:], T.rv[:, lo:hi], False, True)))
+
+        def offsets_y(i):
+            need("v", t_o[i])
+            o, lo, hi = offs[i]
+            t_o[i] = run("v", v.tensor_copy(T.off_d[:, lo:hi], o[:, 0:hi - lo]))
+
+        offsets_y(0)
+        landed = sum(GROUPS[place(x, rank)][2] for x in range(N) if x != rank)
+        v.wait_ge(S.arr, landed)
+        a.wait_ge(S.arr, landed)
+        need("v", toks[rank])
+        need("a", toks[rank])
         at, n_y = 0, 0
-        for wy in Y_CHUNKS:
-            for qn in ("v", "a"):
+        for i, ws in enumerate(Y_CHUNKS):
+            if i == 1:
+                offsets_y(1)
+            for wy, qn in zip(ws, ("v", "a")):
                 src = T.win[:].indirect(T.off_d[:, at // 16:(at + wy) // 16])
                 dst = T.out[:, at:at + wy]
+                need(qn, t_o[0] if at + wy <= 16 * Y1 else t_o[1])
                 t = run("v", v.tensor_copy(dst, src)) if qn == "v" else run("a", a.activation(dst, src, COPY))
                 need("s", t)
                 g.sync.dma_start(T.y[:, at:at + wy], dst).then_inc(S.ys, 16)

from concourse.bass import DstId, RemoteDMATransfer
from concourse.mybir import AluOpType, ActivationFunctionType

N, R, CAPP = 16, 8192, 256
NJ, C, K = 8, 32, 16
UP = 3
KA = 11
ND = 4
NCH = 4
W = R // NCH
E, EC = 8, 16
ADD, SUB, MULT, EQ = AluOpType.add, AluOpType.subtract, AluOpType.mult, AluOpType.is_equal
SR, AN = AluOpType.arith_shift_right, AluOpType.bitwise_and
COPY, ABS, RELU = ActivationFunctionType.Copy, ActivationFunctionType.Abs, ActivationFunctionType.Relu
Y_CHUNKS = ((256, 256), (768, 768), (1024, 1024), (1024, 1024), (704, 832), (256, 256))
GROUPS = ((0, 2, 4), (2, 4, 4), (4, 8, 2))
Y1 = 128

SCRATCH = {
    "lst": ("dram", [128, 32], "int32"),
    "lin": ("dram", [256, 32], "int32"),
    "st": ("sbuf", [128, 64], "int32"),
    "uv": ("sbuf", [128, 64], "int32"),
    "key": ("sbuf", [128, 32], "float32"),
    "kabs": ("sbuf", [128, 32 * (K - KA)], "float32"),
    "vi": ("sbuf", [128, 128], "int32"),
    "vb": ("sbuf", [128, 96], "bfloat16"),
    "vf": ("sbuf", [128, 32], "float32"),
    "hot": ("sbuf", [128, 512], "bfloat16"),
    "inc": ("sbuf", [128, 512], "bfloat16"),
    "zz": ("sbuf", [128, 512], "bfloat16"),
    "ww": ("sbuf", [128, 512], "bfloat16"),
    "cnt": ("sbuf", [128, 16], "bfloat16"),
    "cin": ("sbuf", [128, 8 * 16], "bfloat16"),
    "pt": ("sbuf", [128, 32], "float32"),
    "plo": ("sbuf", [128, 32], "float32"),
    "psc": ("sbuf", [128, 32], "float32"),
    "lin2": ("sbuf", [128, 2], "float32"),
    "ones": ("sbuf", [128, 128], "bfloat16"),
    "ends": ("sbuf", [128, 256], "bfloat16"),
    "ident": ("sbuf", [128, 128], "bfloat16"),
    "tri": ("sbuf", [128, 128], "bfloat16"),
    "rst": ("sbuf", [128, 512], "bfloat16"),
    "iota_a": ("sbuf", [128, 128], "bfloat16"),
    "iota_l": ("sbuf", [128, 128], "bfloat16"),
    "iota_b": ("sbuf", [128, 64], "bfloat16"),
    "pc": ("sbuf", [128, 16], "float32"),
    "cdef": ("sbuf", [128, 128], "bfloat16"),
    "bsel": ("sbuf", [128, 128], "bfloat16"),
    "grp": ("sbuf", [128, 128], "bfloat16"),
    "grp128": ("sbuf", [128, 128], "bfloat16"),
    "msk": ("sbuf", [128, 8], "float32"),
    "oh_a": ("sbuf", [128, 32 * 128], "bfloat16"),
    "oh_b": ("sbuf", [128, 64 * 32], "bfloat16"),
    "oh_l": ("sbuf", [128, 8 * 128], "bfloat16"),
    "oh_m": ("sbuf", [128, 8 * 64], "bfloat16"),
    "oh_c": ("sbuf", [128, 8 * 128], "bfloat16"),
    "xi": ("sbuf", [128, 64], "int32"),
    "xlh": ("sbuf", [128, 128], "int32"),
    "xa": ("sbuf", [128, 128], "bfloat16"),
    "xin": ("sbuf", [128, 8 * 128], "bfloat16"),
    "dm": ("sbuf", [128, 16], "bfloat16"),
    "din": ("sbuf", [128, 64], "bfloat16"),
    "duw": ("sbuf", [128, 16], "float32"),
    "xd": ("sbuf", [128, 128], "bfloat16"),
    "xd_in": ("sbuf", [128, 4 * 128], "bfloat16"),
    "ts": ("sbuf", [128, 32], "bfloat16"),
    "rw": ("sbuf", [128, 256], "bfloat16"),
    "ru": ("sbuf", [128, 512], "bfloat16"),
    "rv": ("sbuf", [128, 512], "bfloat16"),
    "off_s": ("sbuf", [128, 128], "uint16"),
    "off_d": ("sbuf", [128, 512], "uint16"),
    "win": ("sbuf", [128, R + N * CAPP], "bfloat16"),
    "gat": ("sbuf", [128, N * CAPP], "bfloat16"),
    "out": ("sbuf", [128, R], "bfloat16"),
}
for _b in ("pb_base", "pb_pos", "pb_x", "pb_hot", "pb_vf", "pb_sum", "pb_wrap"):
    SCRATCH[_b] = ("psum", [128, 512], "float32")

SEMAPHORES = ["qv", "qa", "qp", "qg", "lcopy", "lsent", "la0", "la1", "ld", "loc", "cn", "x_s", "dd", "x_d", "tb",
              "arr", "ys", "tl0", "tl1", "tl2", "tl3"]


def bits(m):
    return [b for b in range(16) if (m >> b) & 1]


def rank_program(g, core, T, topo):
    def chip_of(c):
        return (topo.host(c), topo.chip(c))

    mine = [r for r in range(N) if chip_of(T.cores[r]) == chip_of(core)]
    if not mine:
        return
    rank = mine[0]

    def layout(r):
        me = T.cores[r]
        cs = [c for c in range(256) if chip_of(c) == chip_of(me)]
        far = [c for c in cs if topo.die(c) != topo.die(me)][0]
        return [c for c in cs if c not in (me, far)] + [far, me]

    lay = layout(rank)
    j, last = lay.index(core), NJ - 1
    main, far = lay[NJ - 1], lay[NJ - 2]
    is_main, is_far = core == main, core == far
    sender = is_main or is_far
    S = T.sem
    v, a, p = g.vector, g.scalar, g.tensor
    Q = {"v": v, "a": a, "p": p, "g": g, "s": g.sync}
    cnt = {"v": 0, "a": 0, "p": 0, "g": 0}
    seen = {}

    def run(q, ins):
        ins.then_inc(S["q" + q], 1)
        cnt[q] += 1
        return (q, cnt[q])

    def need(q, *toks):
        best = {}
        for t in toks:
            best[t[0]] = max(best.get(t[0], 0), t[1])
        for s, n in best.items():
            if seen.get((q, s), 0) < n:
                Q[q].wait_ge(S["q" + s], n)
                seen[(q, s)] = n

    def place(x, d):
        at = (d - x - 1) % 8
        return [i for i, y in enumerate(GROUPS) if y[0] <= at < y[1]][0]

    def did(d):
        rid, pid = topo.addr(d, core)
        return DstId(rid=rid, pnc=pid)

    def engines(dsts, n, first=0):
        m = 0xFFFF
        for d in dsts:
            m &= topo.mask(core, d)
        return sum(1 << x for x in bits(m)[first:first + n])

    loc = [0]

    def move(src, dst, dsts, sem, n, first=0):
        return RemoteDMATransfer(dst_ids=[did(d) for d in dsts], dma_engine_mask=engines(dsts, n, first), remote_sem=sem,
                                 srcs=[src], dsts=[dst for _ in dsts], alu_op=0)

    def send(parts, local=None):
        g.remote_dma_fused([move(*x) for x in parts], local_sem=S.loc if local is None else local)
        if local is None:
            loc[0] += sum(x[4] for x in parts)

    def others(cs):
        return [c for c in cs if c != core]

    def iota(out, pattern, base, cm):
        return run("g", g.iota(out, pattern, base, cm, allow_small_or_imprecise_dtypes=True))

    def load_tab(i):
        g.sync.dma_start(T.win[:, W * i:W * i + W], T.tab[:, W * i:W * i + W]).then_inc(S["tl%d" % i], 16)

    if is_main:
        g.sync.dma_start(T.lst[0:64, :], T.src[:]).then_inc(S.lcopy, 16)
        g.scalar.dma_start(T.lst[64:128, :], T.dst[:]).then_inc(S.lcopy, 16)
        load_tab(0)
    t_ones = run("v", v.memset(T.ones[:], 1.0))
    t_r = run("v", v.memset(T.rst[:], 1.0))
    need("v", t_r)
    t_r = run("v", v.memset(T.rst[:, 0::C], 0.0))
    if sender:
        t_k = run("v", v.memset(T.msk[:], 1.0))
    ends = [(slice(0, 64), True), (slice(64, 128), False)] if is_main else [(slice(0, 128), j < UP)]
    for rows, up in ends:
        run("v", v.memset(T.lin2[rows, 0:1], 255.0 / 128.0 if up else -255.0 / 128.0))
        run("v", v.memset(T.lin2[rows, 1:2], 1.0 if up else 256.0))
        k_a = iota(T.iota_a[rows, :], [[1 if up else -1, 128]], 1 if up else 128, 0)
        if is_main:
            need("g", k_a)
    if is_main:
        run("v", v.memset(T.ends[:, 0:64], 1.0))
        run("v", v.memset(T.ends[:, 64:192], 0.0))
        t_ones = run("v", v.memset(T.ends[:, 192:256], 1.0))
    need("g", t_ones)
    k_i = run("g", g.affine_select(T.ident[:], T.ones[:], [[-1, 128]], EQ, 0.0, 0, 1))
    if is_main:
        k = rank % 2
        dsts = others([layout((rank + 1 + h) % N)[rank // 2] for h in range(N)])
        g.wait_ge(S.lcopy, 32)
        send([(T.lst[:], T.lin[128 * k:128 * k + 128, :], dsts, S["la%d" % k], E)], S.lsent)
    k_t = run("g", g.affine_select(T.tri[:], T.ones[:], [[1, 128]], AluOpType.is_gt, 0.0, 0, -1))
    if is_main:
        need("v", k_t)
        k_t = run("v", v.memset(T.tri[0:64, 64:128], 0.0))
    if sender:
        k_s = run("g", g.affine_select(T.bsel[:], T.ones[:], [[0, 8], [-1, 16]], EQ, 0.0, 0, 1))
        need("g", t_k)
        k_m = run("g", g.affine_select(T.msk[:], T.msk[:], [[-16, 8]], AluOpType.is_ge, 0.0, 0, 1))
        need("g", k_m)
        k_m = run("g", g.affine_select(T.msk[:], T.msk[:], [[16, 8]], AluOpType.is_ge, 0.0, 15, -1))
        need("p", k_s)
        pt = run("p", p.matmul(T.pb_wrap[:, 0:128], T.bsel[:], T.bsel[:], True, True))
        need("v", pt)
        run("v", v.tensor_copy(T.grp[:], T.pb_wrap[:, 0:128]))
        t_g = run("v", v.tensor_scalar(T.grp128[:], T.pb_wrap[:, 0:128], 128.0, None, MULT))
    if is_main:
        iota(T.cdef[:, 0:64], [[0, 64]], 0, 1)
        k_c = iota(T.cdef[:, 64:128], [[1, 64]], 0, 0)
    if j < ND:
        iota(T.iota_l[:], [[1, 128]], 0, 0)
        iota(T.iota_b[:], [[1, 64]], 1, 0)
        iota(T.pc[:, 8:16], [[1, 8]], R // 128 + 1 + 8 * j, 0)
        k_p = iota(T.pc[:, 0:8], [[0, 8]], 0, 1)
    for k in range(2):
        q = g.sync if k == 0 or is_main else g.scalar
        if is_main and rank == 2 * j + k:
            s_in, d_in = T.src[:], T.dst[:]
        else:
            q.wait_ge(S["la%d" % k], E)
            s_in, d_in = T.lin[128 * k:128 * k + 64, :], T.lin[128 * k + 64:128 * k + 128, :]
        q.dma_start(T.st[64 * k:64 * k + 64, 0:32], s_in).then_inc(S.ld, 16)
        q.dma_start(T.st[64 * k:64 * k + 64, 32:64], d_in).then_inc(S.ld, 16)
    if is_main:
        g.sync.wait_ge(S.lsent, E)
        for i in range(1, NCH):
            load_tab(i)
        for i in range(NCH):
            g.wait_ge(S["tl%d" % i], 16)
            send([(T.win[:, W * i:W * i + W], T.win[:, W * i:W * i + W], [far], S.tb, 16)])

    v.wait_ge(S.ld, 64)
    t1 = run("v", v.tensor_scalar(T.uv[:, 0:32], T.st[:, 0:32], 8, 480, SR, AN))
    t2 = run("v", v.tensor_scalar(T.uv[:, 32:64], T.st[:, 32:64], 13, None, SR))
    need("v", t1, t2)
    t = run("v", v.tensor_tensor(T.key[:], T.uv[:, 0:32], T.uv[:, 32:64], ADD))
    need("v", t)
    need("a", t)
    for k in range(KA):
        t_m = run("v", v.tensor_scalar(T.hot[:, C * k:C * k + C], T.key[:], float(32 * rank + k), None, EQ))
    for k in range(KA, K):
        t = run("a", a.activation(T.kabs[:, C * (k - KA):C * (k - KA) + C], T.key[:], ABS, bias=-float(32 * rank + k)))
    need("a", t)
    a_m = run("a", a.activation(T.hot[:, C * KA:C * K], T.kabs[:], RELU, bias=1.0, scale=-1.0))
    need("v", t_m, a_m, t_r)
    t_q = run("v", v.tensor_tensor_scan(T.inc[:], T.rst[:], T.hot[:], 0.0, MULT, ADD))
    need("v", t_q)
    t_c = run("v", v.tensor_copy(T.cnt[:], T.inc[:, C - 1::C]))
    if j < last:
        need("g", t_c)
        send([(T.cnt[:], T.cin[:, K * j:K * j + K], (lay[j + 1:UP] if j < UP else lay[j + 1:last]) + [main], S.cn, EC)])
    need("p", t_m, a_m, k_i)
    p_h = run("p", p.matmul(T.pb_hot[:], T.ident[:], T.hot[:], True, True))
    t = run("v", v.tensor_scalar(T.vi[:, 96:128], T.st[:, 32:64], 7, 63, SR, AN))
    run("v", v.tensor_scalar(T.vi[:, 0:32], T.st[:, 0:32], 127, None, AN))
    run("v", v.tensor_scalar(T.vi[:, 32:64], T.st[:, 0:32], 7, 63, SR, AN))
    t1 = run("v", v.tensor_scalar(T.vi[:, 64:96], T.st[:, 32:64], 127, None, AN))
    need("v", t)
    t_vf = run("v", v.tensor_scalar(T.vf[:], T.vi[:, 96:128], 1.0, None, ADD))
    need("v", t1)
    t_vb = run("v", v.tensor_copy(T.vb[:], T.vi[:, 0:96]))
    need("a", t_vf, t_m, a_m)
    a_b = []
    for c in range(C):
        a_b.append(run("a", a.activation(T.oh_b[:, C * 48 + c:C * 64:C], T.hot[:, c::C], COPY, scale=T.vf[:, c:c + 1])))
    need("p", t_vb)
    for kind in range(3):
        for i in range(2):
            p_v = run("p", p.matmul(T.pb_vf[:, 64 * kind + 32 * i:64 * kind + 32 * i + 32], T.ident[:],
                                    T.vb[:, 32 * kind:32 * kind + 32], True, True))
    need("v", p_h)
    t_z = run("v", v.tensor_tensor(T.zz[:], T.inc[:], T.pb_hot[:], MULT))
    need("v", p_v)
    for kind in range(3):
        for k in range(0, K, 2):
            row = 16 * (k // 8) + 8 * kind + k % 8 if kind < 2 else 32 + k
            t_b = run("v", v.tensor_tensor(T.oh_b[:, C * row:C * row + 2 * C], T.hot[:, C * k:C * k + 2 * C],
                                           T.pb_vf[:, 64 * kind:64 * kind + 64], MULT))
    need("p", t_z)
    for k in range(K):
        run("p", p.matmul(T.pb_pos[:, 0:C], T.ident[:], T.zz[:, C * k:C * k + C], k == 0, False))
    before = list(range(last)) if is_main else list(range(j)) if j < UP else list(range(UP, j))
    need("p", t_c, k_t, t_ones)
    p_b = run("p", p.matmul(T.pb_base[:, 0:K], T.tri[:], T.cnt[:], True, not before))
    if before:
        p.wait_ge(S.cn, EC * len(before))
        for i in before:
            lhs = T.ones[:] if not is_main else T.ends[:, 0:128] if i < UP else T.ends[:, 128:256]
            p_b = run("p", p.matmul(T.pb_base[:, 0:K], lhs, T.cin[:, K * i:K * i + K], False, i == before[-1]))
    need("v", p_b)
    for k in range(K):
        t = run("v", v.tensor_scalar(T.ww[:, C * k:C * k + C], T.hot[:, C * k:C * k + C], T.pb_base[:, k:k + 1], None, MULT))
        need("p", t)
        p_t = run("p", p.matmul(T.pb_pos[:, 0:C], T.ident[:], T.ww[:, C * k:C * k + C], False, k == K - 1))
    need("v", p_t)
    t = run("v", v.tensor_scalar(T.pt[:], T.pb_pos[:, 0:C], 128.0, 128.0, AluOpType.is_gt, MULT))
    need("v", t)
    run("v", v.tensor_tensor(T.plo[:], T.pb_pos[:, 0:C], T.pt[:], SUB))
    t_pos = run("v", v.tensor_scalar(T.psc[:], T.pt[:], T.lin2[:, 0:1], T.lin2[:, 1:2], MULT, ADD))
    need("v", t_pos, k_a)
    need("p", t_b)
    for c in range(C):
        t = run("v", v.tensor_scalar(T.oh_a[:, 128 * c:128 * c + 128], T.iota_a[:], T.plo[:, c:c + 1], T.psc[:, c:c + 1],
                                     EQ, MULT))
        need("p", t, a_b[c])
        p_x = run("p", p.matmul(T.pb_x[:, 0:64], T.oh_a[:, 128 * c:128 * c + 128], T.oh_b[:, c::C], c == 0, c == C - 1))
    need("v", p_x)
    t = run("v", v.tensor_copy(T.xi[:], T.pb_x[:, 0:64]))
    need("v", t)
    t1 = run("v", v.tensor_scalar(T.xlh[:, 0:64], T.xi[:], 255, None, AN))
    t2 = run("v", v.tensor_scalar(T.xlh[:, 64:128], T.xi[:], 8, None, SR))
    need("v", t1)
    run("v", v.tensor_copy(T.xa[:, 0::2], T.xlh[:, 0:64]))
    need("v", t2)
    t_x = run("v", v.tensor_copy(T.xa[:, 1::2], T.xlh[:, 64:128]))
    need("g", t_x)
    send([(T.xa[:], T.xin[:, 128 * j:128 * j + 128], others([main, far] + lay[:ND]), S.x_s, EC)])

    def total(o, parts):
        for i, x in enumerate(parts):
            t = run("p", p.matmul(o, T.ident[:], x, i == 0, i == len(parts) - 1))
        return t

    if sender:
        hf = rank // 8 if is_main else 1 - rank // 8
        need("p", t_x)
        p.wait_ge(S.x_s, EC * (NJ - 1))
        pt = total(T.pb_sum[:, 0:32], [T.xa[:, 32 * hf:32 * hf + 32] if i == j else
                                       T.xin[:, 128 * i + 32 * hf:128 * i + 32 * hf + 32] for i in range(NJ)])
        need("v", pt, k_m)
        t_t = run("v", v.tensor_copy(T.ts[:], T.pb_sum[:, 0:32]))
        need("v", t_t)
        need("a", t_t, k_m)
        for k in range(0, 8, 2):
            t1 = run("v", v.tensor_scalar(T.rw[:, k::8], T.ts[:], T.msk[:, k:k + 1], None, MULT))
            a1 = run("a", a.activation(T.rw[:, k + 1::8], T.ts[:], COPY, scale=T.msk[:, k + 1:k + 2]))
        need("p", t1, a1, t_g)
        run("p", p.matmul(T.pb_wrap[:, 0:128], T.grp[:], T.rw[:, 0:128], True, False))
        pt = run("p", p.matmul(T.pb_wrap[:, 0:128], T.grp128[:], T.rw[:, 128:256], False, True))
        need("v", pt)
        half = list(range(8 * hf, 8 * hf + 8))
        first = rank % 8 + 1
        peers = half[first:] + half[:first]

        def offsets(xs):
            xs = sorted(x % 8 for x in xs)
            while xs:
                n = 1
                while n < len(xs) and xs[n] == xs[0] + n:
                    n += 1
                at = 16 * xs[0]
                t = run("v", v.tensor_copy(T.off_s[:, at:at + 16 * n], T.pb_wrap[:, at:at + 16 * n]))
                xs = xs[n:]
            return t

        t = offsets(peers[0:2])
        for q in (v, a):
            if is_main:
                for i in range(NCH):
                    q.wait_ge(S["tl%d" % i], 16)
            else:
                q.wait_ge(S.tb, 16 * NCH)
        toks = {}
        for i in range(0, 8, 2):
            for x, qn in ((peers[i], "v"), (peers[i + 1], "a")):
                dst = T.win[:, R + CAPP * x:R + CAPP * x + CAPP] if x == rank else T.gat[:, CAPP * x:CAPP * x + CAPP]
                src = T.win[:, 0:R].indirect(T.off_s[:, 16 * (x % 8):16 * (x % 8) + 16])
                need(qn, t)
                toks[x] = run("v", v.tensor_copy(dst, src)) if qn == "v" else run("a", a.activation(dst, src, COPY))
            if i == 0:
                t = offsets(peers[2:])
        for i0, i1, n in GROUPS:
            grp = [x for x in peers[i0:i1] if x != rank]
            need("g", *[toks[x] for x in grp])
            send([(T.gat[:, CAPP * x:CAPP * x + CAPP], T.win[:, R + CAPP * rank:R + CAPP * rank + CAPP], [T.cores[x]], S.arr,
                   n, n * i2) for i2, x in enumerate(grp)])

    if j < ND:
        need("p", t_x)
        p.wait_ge(S.x_s, EC * (NJ - 1))
        pt = total(T.pb_sum[:, 0:64], [T.xa[:, 64:128] if i == j else T.xin[:, 128 * i + 64:128 * i + 128] for i in range(NJ)])
        need("v", pt)
        run("v", v.tensor_copy(T.dm[:, 0:8], T.pb_sum[:, 8 * j:8 * j + 8]))
        t_dm = run("v", v.tensor_copy(T.dm[:, 8:16], T.pb_sum[:, 32 + 8 * j:40 + 8 * j]))
        need("g", t_dm)
        me = rank % 4
        parts = []
        for i in range(4):
            d = layout(4 * j + i)[rank // 4]
            if d != core:
                parts.append((T.dm[:], T.din[:, 16 * me:16 * me + 16], [d], S.dd, 2, 2 * i))
        send(parts)
        own = rank // 4 == j
        need("v", t_dm, k_p)
        if own:
            t = run("v", v.tensor_copy(T.din[:, 16 * me:16 * me + 16], T.dm[:]))
            need("v", t)
        v.wait_ge(S.dd, 2 * (3 if own else 4))
        for b in range(2):
            run("v", v.tensor_scalar(T.duw[:, b:8:2], T.din[:, 2 * me + b::16], -1.0, T.pc[:, 0:1], MULT, ADD))
            t_d = run("v", v.tensor_tensor(T.duw[:, 8 + b::2], T.pc[:, 8 + b::2], T.din[:, 8 + 2 * me + b::16], SUB))
        need("a", t_d)
        for i in range(4):
            for b in range(2):
                x, at = 2 * i + b, 16 * i + 2 * me + b
                t = run("v", v.tensor_scalar(T.oh_m[:, 64 * x:64 * x + 64], T.iota_b[:], T.din[:, at + 8:at + 9], None, EQ))
                t1 = run("v", v.tensor_scalar(T.oh_l[:, 128 * x:128 * x + 128], T.iota_l[:], T.din[:, at:at + 1], None, EQ))
                need("a", t)
                run("a", a.activation(T.oh_c[:, 128 * x:128 * x + 64], T.oh_m[:, 64 * x:64 * x + 64], COPY,
                                      scale=T.duw[:, x:x + 1]))
                a1 = run("a", a.activation(T.oh_c[:, 128 * x + 64:128 * x + 128], T.oh_m[:, 64 * x:64 * x + 64], COPY,
                                           scale=T.duw[:, 8 + x:9 + x]))
                need("p", t1, a1)
                p_x = run("p", p.matmul(T.pb_wrap[:, 0:128], T.oh_l[:, 128 * x:128 * x + 128],
                                        T.oh_c[:, 128 * x:128 * x + 128], x == 0, x == 7))
        need("v", p_x)
        t = run("v", v.tensor_copy(T.xd[:], T.pb_wrap[:, 0:128]))
        need("g", t)
        send([(T.xd[:], T.xd_in[:, 128 * j:128 * j + 128], [main], S.x_d, E)])

    if is_main:
        need("p", k_c, t_t)
        p.wait_ge(S.x_d, E * ND)
        p_u, p_w = [total(o[:, 0:64], [T.xd_in[:, 128 * i + h:128 * i + h + 64] for i in range(ND)] + [T.cdef[:, h:h + 64]])
                    for o, h in ((T.pb_sum, 0), (T.pb_pos, 64))]
        need("v", p_u)
        need("a", p_w)
        for k in range(8):
            t_u = run("v", v.tensor_scalar(T.ru[:, k::8], T.pb_sum[:, 0:64], T.msk[:, k:k + 1], None, MULT))
            a_w = run("a", a.activation(T.rv[:, k::8], T.pb_pos[:, 0:64], COPY, scale=T.msk[:, k:k + 1]))
        need("p", t_u, a_w)
        t_o, offs = [], ((T.pb_x, 0, Y1), (T.pb_hot, Y1, R // 16))
        for o, lo, hi in offs:
            run("p", p.matmul(o[:, 0:hi - lo], T.grp[:], T.ru[:, lo:hi], True, False))
            t_o.append(run("p", p.matmul(o[:, 0:hi - lo], T.grp128[:], T.rv[:, lo:hi], False, True)))

        def offsets_y(i):
            need("v", t_o[i])
            o, lo, hi = offs[i]
            t_o[i] = run("v", v.tensor_copy(T.off_d[:, lo:hi], o[:, 0:hi - lo]))

        offsets_y(0)
        landed = sum(GROUPS[place(x, rank)][2] for x in range(N) if x != rank)
        v.wait_ge(S.arr, landed)
        a.wait_ge(S.arr, landed)
        need("v", toks[rank])
        need("a", toks[rank])
        at, n_y = 0, 0
        for i, ws in enumerate(Y_CHUNKS):
            if i == 1:
                offsets_y(1)
            for wy, qn in zip(ws, ("v", "a")):
                src = T.win[:].indirect(T.off_d[:, at // 16:(at + wy) // 16])
                dst = T.out[:, at:at + wy]
                need(qn, t_o[0] if at + wy <= 16 * Y1 else t_o[1])
                t = run("v", v.tensor_copy(dst, src)) if qn == "v" else run("a", a.activation(dst, src, COPY))
                need("s", t)
                g.sync.dma_start(T.y[:, at:at + wy], dst).then_inc(S.ys, 16)
                at, n_y = at + wy, n_y + 1
        g.wait_ge(S.ys, 16 * n_y)

    for q in ("v", "a", "p", "g"):
        if cnt[q]:
            g.wait_ge(S["q" + q], cnt[q])
    g.wait_ge(S.loc, loc[0])
